import numpy as np, ml_dtypes
CORES = [3,7,11,15,131,135,139,143]
N = 8
import mx_ref
BF = ml_dtypes.bfloat16
def cut(t, i, w=512):
    return t[:, w * i:w * i + w]
def tile(rs):
    return np.stack(rs, axis=2).reshape(128, -1).astype(BF)
def pick(q, e):
    c = np.concatenate([q[0].reshape(128, -1, 4), np.zeros((128, 1, 4), np.uint8)], axis=1); s = np.concatenate([q[1], np.ones((16, 1), np.uint8)], axis=1)
    return (np.ascontiguousarray(c[:, e].reshape(128, -1)), np.ascontiguousarray(s[:, e]))
def join(*qs):
    return (np.concatenate([q[0] for q in qs], axis=1), np.concatenate([q[1] for q in qs], axis=1))
def put(q, e, v):
    c, s = q[0].reshape(128, -1, 4).copy(), q[1].copy(); c[:, e] = v[0].reshape(128, -1, 4); s[:, e] = v[1]
    return (c.reshape(128, -1), s)
def pk(c, s):
    return (np.ascontiguousarray(c), mx_ref.live(s))
def emit(q):
    return q[0], q[1]
def f(rng, *shape):
    return mx_ref.flush((rng.standard_normal(shape, dtype=np.float32) * np.exp2(rng.integers(-2, 3, shape[:-1] + (1,)))).astype(BF))
def wide(rng, *shape, cols=0):
    v = rng.standard_normal(shape, dtype=np.float32) * np.exp2(rng.integers(-12, 13, shape)).astype(np.float32)
    if cols: v *= np.repeat(np.exp2(rng.integers(-cols, cols + 1, shape[:-2] + (1, shape[-1] // 4))) * (rng.random(shape[:-2] + (1, shape[-1] // 4)) > 0.0625), 4, axis=-1).astype(np.float32)
    return mx_ref.flush(v.astype(BF))
T, G, CS, R = 64, 64, 16, 3
def game(x, qx, w, u):
    wq = [[mx_ref.quantize(np.ascontiguousarray(cut(w[r], i))) for i in range(4)] for r in range(N)]
    uq = [mx_ref.quantize(np.ascontiguousarray(u[r])) for r in range(N)]
    wait = join(*[mx_ref.quantize(np.ascontiguousarray(qx[m])) for m in range(N)])
    s = [mx_ref.quantize(np.ascontiguousarray(x[r])) for r in range(N)]
    num = [r * T + np.arange(T) for r in range(N)]
    log, said, made, head = [[] for r in range(N)], [[] for r in range(N)], [], 0
    for t in range(R):
        for r in range(N):
            a = tile([np.maximum(mx_ref.matmul(wq[r][i], s[r]), np.float32(0)) * np.float32(0.0625) for i in range(4)])
            made.append(a)
            s[r] = mx_ref.quantize(a)
            h = mx_ref.matmul(uq[r], s[r])[:2] + np.float32(0)
            stop = np.flatnonzero(h[0] > h[1])[:CS]
            if stop.size == 0: continue
            log[r].append(pick(s[r], stop))
            said[r].extend(num[r][stop].tolist())
            g = head + np.arange(stop.size)
            s[r] = put(s[r], stop, pick(wait, G * (g % N) + g // N))
            num[r][stop] = N * T + g
            head += stop.size
    return log, said, s, num, made
def fit(d, top=2.0 ** 30):
    try:
        with np.errstate(all="ignore"):
            a = np.abs(np.stack(game(d["x"], d["qx"], d["w"], d["u"])[4]).astype(np.float32))
    except Exception: return False
    return bool(np.isfinite(a).all() and ((a == 0) | (a >= 2.0 ** -30) & (a <= top)).all())
def first(make, top=2.0 ** 30):
    for i in range(5):
        d = make()
        if fit(d, top): break
    return d
def plain(rng):
    w = np.rint(rng.standard_normal((N, 128, 2048), dtype=np.float32) * 8) * 0.125 * np.exp2(rng.integers(-1, 2, (N, 128, 1))) + 0.0
    u = np.zeros((N, 128, 512), np.float32)
    u[:, :, :8] = rng.standard_normal((N, 128, 8))
    u[:, :, 4:8] += 0.15 * rng.random((N, 1, 1))
    u *= np.exp2(rng.integers(-1, 2, (N, 128, 1)))
    return {"x": np.array(f(rng, N, 128, 4 * T)), "qx": np.array(f(rng, N, 128, 4 * G)), "w": w.astype(BF), "u": np.array(mx_ref.flush(u.astype(BF))), "v": np.array(f(rng, N, 128, 512))}
def channel(w, alone=False):
    a = w.astype(np.float32).reshape(N, 128, 4, 128, 4)
    if alone: a[:, :8] = 0
    a[:, :, :, :8, :] = 0
    for i in range(4):
        for j in range(8): a[:, j, i, j, i] = 16
    return a.reshape(N, 128, 2048).astype(BF)
def flags(d, live, wait):
    d["x"][:, :8] = np.repeat(np.where(live, 4.0, 0.0), 4, axis=1)[:, None, :].astype(BF)
    d["qx"][:, :8] = np.repeat(np.where(wait.reshape(G, N).T, 4.0, 0.0), 4, axis=1)[:, None, :].astype(BF)
def signed(t, a, b):
    o = np.abs(t.astype(np.float32))
    o[:, :4] *= a
    o[:, 4:8] *= b
    return o.astype(BF)
def setup_inputs(rng):
    return first(lambda: plain(rng), 2.0 ** 8)
def setup_inputs_many(rng):
    def make():
        d = plain(rng)
        d["w"] = channel(d["w"])
        pair = rng.integers(0, 2, N * G // 2)
        flags(d, np.stack([rng.permutation(T) < 3 * T // 4 for r in range(N)]), np.stack([pair, 1 - pair], axis=1).reshape(-1) == 1)
        for r in range(N):
            a = np.zeros((128, 512), np.float32)
            a[:8, :4] = 1
            a[8:, 4:8] = np.abs(rng.standard_normal((120, 4))) * 2.0 ** -8
            d["u"][r] = mx_ref.flush(a.astype(BF))
        return d
    return first(make)
def setup_inputs_none(rng):
    def make():
        d = plain(rng)
        a, b = rng.permutation(N)[:2]
        d["u"][a] = signed(d["u"][a], -1, 1)
        d["u"][b] = signed(d["u"][b], 1, -1)
        return d
    return first(make)
def setup_inputs_ties(rng):
    def make():
        d = plain(rng)
        d["w"] = channel(d["w"])
        flags(d, np.stack([rng.permutation(T) < T // 3 for r in range(N)]), rng.random(N * G) < 0.3)
        d["u"][:, :, 4:8] = d["u"][:, :, :4]
        d["u"][:, :8, :4] = 1
        d["u"][:, :8, 4:8] = 0
        a, c = rng.permutation(N)[:2]
        d["u"][a, :, 4:8] = d["u"][a, :, :4]
        d["u"][c] = 0
        d["u"][c, :7, :8] = 1
        d["u"][c, 7, :4] = 2.0 ** -8
        d["u"][c, 7, 4:8] = 2.0 ** -9
        return d
    return first(make)
def setup_inputs_zero(rng):
    def make():
        d = plain(rng)
        d["w"] = channel(d["w"], alone=True)
        live = np.stack([rng.permutation(np.repeat([0, 1, 2], [T - 2 * (T // 8), T // 8, T // 8])) for r in range(N)])
        for k, e in (("x", live), ("qx", rng.choice(3, (N, G), p=[0.75, 0.125, 0.125]))):
            m = np.repeat(e, 4, axis=1)[:, None, :]
            c = np.where(m == 0, d[k].astype(np.float32), np.float32(0))
            c[:, :8] = np.where(m == 2, np.float32(-4), c[:, :8])
            d[k] = c.astype(BF)
        for r in rng.permutation(N)[:N // 2]: d["u"][r] = signed(d["u"][r], 1, -1)
        return d
    return first(make)
def setup_inputs_spread(rng):
    return first(lambda: {**plain(rng), "x": wide(rng, N, 128, 4 * T, cols=6), "qx": wide(rng, N, 128, 4 * G, cols=6)})
def check_inputs(d):
    b = []
    for k in ("x", "qx", "w", "u", "v"):
        a = np.abs(d[k].astype(np.float32))
        if not (np.isfinite(a).all() and ((a == 0) | (a >= 2.0 ** -30) & (a <= 2.0 ** 30)).all()): b.append("a value of " + k)
    if (d["u"][:, :, 8:].astype(np.float32) != 0).any(): b.append("u has numbers behind its first two columns")
    if not b and not fit(d): b.append("a number that a layer makes")
    return b
def reference(x, qx, w, u, v):
    log, said, s, num, made = game(x, qx, w, u)
    M = R * CS + T
    oc, osc = np.zeros((N, 128, 4 * M), np.uint8), np.zeros((N, 16, M), np.uint8)
    sid, y = np.full((N, 1, M), -1, np.float32), np.zeros((N, 128, T), np.float32)
    for r in range(N):
        n = len(said[r])
        oc[r], osc[r] = emit(pick(join(*log[r], s[r]), np.concatenate([np.arange(n), np.full(R * CS - n, -1), n + np.arange(T)])))
        sid[r, 0, :n] = said[r]
        sid[r, 0, R * CS:] = num[r]
        y[r] = mx_ref.matmul(mx_ref.quantize(np.ascontiguousarray(v[r])), s[r])
    return {"oc": oc, "osc": osc, "sid": sid, "y": y}

@@ -1,0 +1,431 @@
+from concourse.bass import DstId, RemoteDMATransfer
+from concourse.mybir import dt, AluOpType, AxisListType, ActivationFunctionType
+
+NR, PL, CS, RD = 8, 64, 16, 3
+USED = RD * CS
+BASE, SH = 144, 9
+QW = 1 << (SH - 1)
+ZW = BASE + 3 * QW + 16
+
+SCRATCH = {
+    "wt": ("sbuf", [128, 2048], "bfloat16"), "xt": ("sbuf", [128, 512], "bfloat16"),
+    "qt": ("sbuf", [128, 512], "bfloat16"), "ut": ("sbuf", [128, 512], "bfloat16"), "vt": ("sbuf", [128, 512], "bfloat16"),
+    "fl": ("sbuf", [128, 3000], "float32"), "il": ("sbuf", [128, 256], "int32"), "ol": ("sbuf", [128, 128], "uint16"),
+    "sidc": ("sbuf", [128, 96], "float32"), "sidl": ("sbuf", [128, 48], "float32"), "ys": ("sbuf", [128, 64], "float32"),
+    "ha": ("psum", [128, 512], "float32"), "py": ("psum", [128, 512], "float32"),
+}
+for _n, _w in (("wc", 512), ("uq", 128), ("ua", 128), ("ub", 128), ("vq", 128), ("wq", 256), ("cc", 128), ("lg", 48),
+               ("x0", 128), ("x1", 128), ("x2", 128), ("x3", 128), ("z0", ZW), ("z1", ZW), ("z2", ZW)):
+    SCRATCH[_n] = ("sbuf", [128, _w], "float8_e4m3fn_x4")
+    SCRATCH[_n + "s"] = ("sbuf", [128, _w], "uint8")
+for _t in range(RD):
+    SCRATCH["at%d" % _t] = ("sbuf", [128, 512], "bfloat16")
+    SCRATCH["sat%d" % _t] = ("sbuf", [128, 72], "bfloat16")
+    SCRATCH["cnt%d" % _t] = ("sbuf", [128, 8], "bfloat16")
+for _t in range(RD + 1):
+    SCRATCH["num%d" % _t] = ("sbuf", [128, 72], "float32")
+    SCRATCH["pz%d" % _t] = ("psum", [128, 512], "float32")
+SEMAPHORES = ["vs", "ss", "ts", "gs", "lqx", "lu", "lx", "lv", "lw0", "lw1", "st", "pre", "loc"]
+SEMAPHORES += [k + str(t) for k in ("ac", "ah", "ak", "ap") for t in range(RD)]
+
+
+def rank_program(g, core, T, topo):
+    rank = T.rank_of(core)
+    if rank is None:
+        return
+    A, AF = AluOpType, ActivationFunctionType
+    v, s, te, sy = g.vector, g.scalar, g.tensor, g.sync
+    u8, u32 = dt.uint8, dt.uint32
+
+    def quad_of(c):
+        return [d for d in T.cores if d in topo.cores_of(c) or topo.mates(c, d)]
+
+    quad = quad_of(core)
+    me = quad.index(core)
+    mate = [d for d in quad if d in topo.cores_of(core) and d != core][0]
+    side = [d for d in quad if d not in topo.cores_of(core)]
+    other = [d for d in T.cores if d not in quad]
+    twin = [d for d in other if topo.same_plane(core, d) and topo.die(d) == topo.die(core)][0]
+    half = 0 if rank < T.rank_of(twin) else 1
+    r0 = T.rank_of(quad[0])
+    peers = [quad[(me + e) % 4] for e in range(4)]
+    eoff = topo.engines(core, side[0])
+    eon = [e for e in topo.engines(core, mate) if e not in eoff][::2]
+
+    def urgent(sr, d):
+        return sr < max(T.rank_of(c) for c in quad_of(d))
+
+    def wanted(sr, d, t):
+        return t < RD - 1 or urgent(sr, d)
+
+    def early(sr, d):
+        return urgent(sr, d) or T.cores[sr] in quad_of(d)
+
+    def bits(es):
+        return sum(1 << e for e in es)
+
+    def did(d):
+        rid, pid = topo.addr(d, core)
+        return DstId(rid=rid, pnc=pid)
+
+    Q = {"v": v, "s": s, "t": te, "g": g, "y": sy}
+    own = {"v": "vs", "s": "ss", "t": "ts", "g": "gs"}
+    done = {"vs": 0, "ss": 0, "ts": 0, "gs": 0}
+    dmas = {}
+    seen = {q: {} for q in Q}
+
+    def need(q, deps):
+        top = {}
+        for n, c in deps:
+            top[n] = max(top.get(n, 0), c)
+        for n, c in top.items():
+            if seen[q].get(n, 0) < c:
+                Q[q].wait_ge(T.sem[n], c)
+                seen[q][n] = c
+
+    def run(q, deps, call, *a, **k):
+        need(q, deps)
+        n = own[q]
+        call(*a, **k).then_inc(T.sem[n], 1)
+        done[n] += 1
+        return (n, done[n])
+
+    def V(deps, call, *a, **k):
+        return run("v", deps, call, *a, **k)
+
+    def S(deps, call, *a, **k):
+        return run("s", deps, call, *a, **k)
+
+    def dma(q, deps, sem, out, in_):
+        need(q, deps)
+        Q[q].dma_start(out, in_).then_inc(T.sem[sem], 16)
+        dmas[sem] = dmas.get(sem, 0) + 16
+        return (sem, dmas[sem])
+
+    at = {"fl": 0, "il": 0, "ol": 0}
+
+    def take(buf, n):
+        a = at[buf]
+        at[buf] = a + n + (n % 2 if buf == "ol" else 0)
+        return T[buf][:, a:a + n]
+
+    def F(n):
+        return take("fl", n)
+
+    def I(n):
+        return take("il", n)
+
+    def O(n):
+        return take("ol", n)
+
+    tu = dma("s", [], "lu", T.ut[:, 0:8], T.u[:, 0:8])
+    tqx = dma("y", [], "lqx", T.qt[:, 0:4 * USED], T.qx[:, 0:4 * USED])
+    tw0 = dma("s", [], "lw0", T.wt[:, 0:1536], T.w[:, 0:1536])
+    tx = dma("y", [], "lx", T.xt[:, 0:256], T.x[:, :])
+    tw1 = dma("y", [], "lw1", T.wt[:, 1536:2048], T.w[:, 1536:2048])
+    tv = dma("y", [], "lv", T.vt[:, :], T.v[:, :])
+    tw = [tw0, tw0, tw0, tw1]
+
+    def iota(out, pattern, base, cm, fl):
+        if fl:
+            return run("g", [], g.iota, out, pattern, base, cm, allow_small_or_imprecise_dtypes=True)
+        return run("g", [], g.iota, out, pattern, base, cm)
+
+    a0 = at["fl"]
+    neg, rs0, jw0 = F(7), F(64), F(4)
+    ip, ip2, jp = I(1), I(1), I(64)
+    t_ip = iota(ip, [[0, 1]], 0, 1, False)
+    t_ip2 = iota(ip2, [[0, 1]], 4 * me, 1, False)
+    ngs = []
+    if rank < NR - 1:
+        ngs.append(iota(T.fl[:, a0:a0 + 7 - rank], [[1, 7 - rank]], -7, 0, True))
+    if rank > 0:
+        ngs.append(iota(T.fl[:, a0 + 7 - rank:a0 + 7], [[1, rank]], 1 - rank, 0, True))
+    t_jp = iota(jp, [[1, 64]], 0, -1, False)
+    t_rs = iota(rs0, [[0, 4], [1, 16]], 0, 0, True)
+    t_jw0 = iota(jw0, [[16, 4]], 0, 0, True)
+    ca = at["fl"]
+    c16 = F(64)
+    t_c16 = iota(c16, [[0, 64]], 16, 0, True)
+
+    t_qz = V([], v.memset, T.qt[:, 4 * USED:512], 0.0)
+    t_xz = V([], v.memset, T.xt[:, 256:512], 0.0)
+    t_uz = V([], v.memset, T.ut[:, 12:512], 0.0)
+    O(16)
+    V([], v.memset, T.ol[:, 0:8], 0)
+    t_lo = V([], v.memset, T.ol[:, 8:16], 2)
+    nil = T.sat0[:, 0:1]
+    t_nil = V([], v.memset, nil, 0.0)
+    t_un = S([tu], s.activation, T.ut[:, 8:12], T.ut[:, 4:8], AF.Copy, scale=-1.0)
+    t_a0 = S([t_xz], s.activation, T.at0[:, 256:512], T.xt[:, 256:512], AF.Copy)
+    rst, jd, kh, jq16, hd = F(64), F(4), F(1), F(3), F(1)
+    c_rs = S([t_rs], s.activation, rst, rs0, AF.Sign)
+    t_hd = S([t_nil], s.activation, hd, nil, AF.Copy)
+
+    ik, kcol, ic, dcol = I(1), F(1), I(1), F(1)
+    m7a = at["fl"]
+    mask7, sm = F(7), F(1)
+    ih, isl, hc0a, hc0 = I(1), I(1), F(1), F(1)
+    i16, m16 = I(64), F(64)
+    jwa = at["fl"]
+    jw = F(4)
+    jq = T.fl[:, jwa:jwa + 3]
+    c_ik = V([t_ip], v.tensor_scalar, ik, ip, 15, None, A.bitwise_and)
+    c_ic = V([t_ip2], v.tensor_scalar, ic, ip2, 2, 3, A.logical_shift_right, A.bitwise_and)
+    c_ih = V([t_ip], v.tensor_scalar, ih, ip, 1, 1, A.logical_shift_right, A.bitwise_and)
+    c_k = V([c_ik], v.tensor_copy, kcol, ik)
+    c_is = V([t_ip], v.tensor_scalar, isl, ip, 1, None, A.bitwise_and)
+    c_i16 = V([t_jp], v.tensor_scalar, i16, jp, 15, None, A.bitwise_and)
+
+    wb = 128 * half
+    t_wq = V([tqx, t_qz], v.quantize_mx, T.wq[:, wb:wb + 128], T.wqs[:, wb:wb + 128], T.qt[:, :])
+    need("g", [t_wq])
+    rid, pid = topo.addr(twin, core)
+    g.remote_dma(T.wq[:, wb:wb + USED].bitcast(u8), T.wq[:, wb:wb + USED].bitcast(u8), T.sem.pre, T.sem.loc, pid, rid, topo.mask(core, twin))
+    g.remote_dma(T.wqs[:, wb:wb + USED], T.wqs[:, wb:wb + USED], T.sem.pre, T.sem.loc, pid, rid, topo.mask(core, twin))
+    npre = 2 * len(topo.engines(core, twin))
+    sent = [npre]
+    t_num = [iota(T.num0[:, 0:64], [[1, 64]], PL * rank, 0, True)]
+    t_fill = iota(T.sidc[:, :], [[0, 96]], -1, 0, True)
+
+    t_uq = V([tu, t_uz, t_un], v.quantize_mx, T.uq[:, :], T.uqs[:, :], T.ut[:, :])
+    c_d = V([c_ic], v.tensor_scalar, dcol, ic, float(r0), None, A.add)
+    t_ub = [V([t_uq, t_lo], v.tensor_copy, T.ub[:, :].bitcast(u32), T.uq[:, :].bitcast(u32).indirect(T.ol[:, 8:16])),
+            S([t_uq, t_lo], s.activation, T.ubs[:, :], T.uqs[:, :].indirect(T.ol[:, 8:16]), AF.Copy)]
+    t_ua = [V([], v.tensor_copy, T.ua[:, :].bitcast(u32), T.uq[:, :].bitcast(u32).indirect(T.ol[:, 0:8])),
+            S([], s.activation, T.uas[:, :], T.uqs[:, :].indirect(T.ol[:, 0:8]), AF.Copy)]
+    c_m16 = V([c_i16], v.tensor_scalar, m16, i16, 0.0, None, A.is_equal)
+    c_jw = V([t_jw0, c_k], v.tensor_scalar, jw, jw0, kcol, None, A.add)
+    c_ha = V([c_ih], v.tensor_scalar, hc0a, ih, 128.0 - 0.5, (3.5 - me) / 8.0, A.mult, A.add)
+    c_kh = S([c_k], s.activation, kh, kcol, AF.Copy, bias=0.5)
+    c_jd = S([c_jw], s.activation, jd, jw, AF.Copy, bias=float(BASE), scale=-1.0)
+    c_j16 = S([], s.activation, jq16, jq, AF.Copy, bias=16.0)
+
+    def quant(i):
+        return V([tw[i]], v.quantize_mx, T.wc[:, 128 * i:128 * i + 128], T.wcs[:, 128 * i:128 * i + 128], T.wt[:, 512 * i:512 * i + 512])
+
+    def zeros(n):
+        return V([t_xz], v.quantize_mx, T[n][:, :], T[n + "s"][:, :], T.xt[:, :])
+
+    t_w = [quant(0)]
+    t_X = [V([tx, t_xz], v.quantize_mx, T.x0[:, :], T.x0s[:, :], T.xt[:, :])]
+    t_w += [quant(i) for i in range(1, 4)]
+
+    hc = hc0
+    counts, t_cf, t_lcs, t_lis = [], [], [], []
+    late, ends, books = {}, [], []
+    for t in range(RD):
+        Xc, Xs = T["x%d" % t], T["x%ds" % t]
+        Zc, Zs = T["z%d" % t], T["z%ds" % t]
+        Nc, Ns = T["x%d" % (t + 1)], T["x%ds" % (t + 1)]
+        At, sat, land = T["at%d" % t], T["sat%d" % t], T["cnt%d" % t]
+        num, numn = T["num%d" % t], T["num%d" % (t + 1)]
+        t_mm = [run("t", t_X + [t_w[i]], te.matmul_mx, T["pz%d" % i][:, 0:128], T.wc[:, 128 * i:128 * i + 128],
+                    T.wcs[:, 128 * i:128 * i + 128], Xc[:, 0:128], Xs[:, 0:128], True, True) for i in range(4)]
+        t_r = []
+        for i in range(4):
+            o, z = At[:, i:256:4], T["pz%d" % i][:, 0:64]
+            if i % 2:
+                t_r.append(V([t_mm[i]], v.tensor_scalar, o, z, 0.0, 0.0625, A.max, A.mult))
+            else:
+                t_r.append(S([t_mm[i]], s.activation, o, z, AF.Relu, scale=0.0625))
+        t_z = V(t_r + [t_a0], v.quantize_mx, Zc[:, 0:128], Zs[:, 0:128], At[:, :])
+        if t == 0:
+            c_m7 = V(ngs + [c_d], v.tensor_scalar, mask7, neg, dcol, 0.0, A.add, A.is_gt)
+            c_sm = V([c_d], v.tensor_scalar, sm, dcol, float(rank), 0.125, A.is_gt, A.mult)
+            t_hc = V([c_ha, c_is], v.tensor_tensor, hc0, hc0a, isl, A.add)
+            for k in range(RD):
+                t_nf = S([t_c16], s.activation, T["num%d" % k][:, 64:72], T.fl[:, ca:ca + 8], AF.Copy, scale=-0.0625)
+            for k in range(1, RD):
+                S([t_nil], s.activation, T["sat%d" % k][:, 0:1], nil, AF.Copy)
+            for k in range(1, RD):
+                t_a0 = S([t_xz], s.activation, T["at%d" % k][:, 256:512], T.xt[:, 256:512], AF.Copy)
+        run("t", [t_z] + t_ua, te.matmul_mx, T.ha[:, 0:128], T.ua[:, :], T.uas[:, :], Zc[:, 0:128], Zs[:, 0:128], True, False)
+        t_h = run("t", t_ub, te.matmul_mx, T.ha[:, 0:128], T.ub[:, :], T.ubs[:, :], Zc[:, 0:128], Zs[:, 0:128], False, True)
+        want, cf = F(64), F(1)
+        t_wn = V([t_h], v.tensor_scalar, want, T.ha[:, 0:64], 0.0, None, A.is_gt)
+        t_sat = V([t_wn, t_c16], v.tensor_tensor_scan, sat[:, 1:65], want, c16, 0.0, A.add, A.min)
+        cown = sat[:, 64:65]
+        need("g", [t_sat])
+        slots = {d: 7 - rank if rank > T.rank_of(d) else 6 - rank for d in side + [mate] + other}
+
+        def give(ds, es):
+            ds = [d for d in ds if wanted(rank, d, t)]
+            if not ds:
+                return []
+            sent.append(len(es))
+            sem = T.sem[("ac%d" if early(rank, ds[0]) else "ah%d") % t]
+            return [RemoteDMATransfer(dst_ids=[did(d) for d in ds], dma_engine_mask=bits(es), remote_sem=sem, srcs=[cown],
+                                      dsts=[land[:, slots[d]:slots[d] + 1] for d in ds])]
+
+        ahead = urgent(rank, other[0])
+        now = give(side + other if ahead else side, eoff) + give([mate], eon)
+        tail = [] if ahead else give(other, eoff)
+        if now:
+            g.remote_dma_fused(now, local_sem=T.sem.loc)
+        inc = {d: len(eon) if d == mate else len(eoff) for d in side + [mate] + other if wanted(T.rank_of(d), core, t)}
+        soon = [d for d in inc if early(T.rank_of(d), core)]
+        na, nac = len(soon), sum(inc[d] for d in soon)
+        nah = sum(inc.values()) - nac
+        hcx, stop, satm, encm, sgn, red = F(1), F(64), F(64), F(64), F(64), F(1)
+        sa = at["fl"]
+        seg, encw = F(64), T.fl[:, sa + 15:sa + 64:16]
+        stopw, nine, wid, wj, tww, hdk, bcol = F(4), F(4), F(4), F(4), F(4), F(1), F(1)
+        logo = O(1)
+        t_rd = S([t_sat, c_kh], s.activation, sgn, sat[:, 1:65], AF.Sign, bias=kh, scale=-1.0, accum_out=red)
+        t_cf.append(S([t_sat], s.activation, cf, cown, AF.Copy))
+        counts.append(cf)
+        if t:
+            tot, hdn, hcn = F(1), F(1), F(1)
+            t_to = V(late[t - 1], v.tensor_reduce, tot, T["cnt%d" % (t - 1)][:, 0:7], AxisListType.X, A.add)
+        t_st = V([t_sat], v.tensor_tensor, stop, sat[:, 1:65], sat[:, 0:64], A.subtract)
+        if t:
+            t_hd = V([t_to, t_hd, t_cf[t - 1]], v.tensor_scalar, hdn, tot, counts[t - 1], hd, A.add, A.add)
+        t_sm = V([c_m16], v.tensor_tensor, satm, sat[:, 1:65], m16, A.mult)
+        if t:
+            t_hc = V([t_hd], v.tensor_scalar, hcn, hdn, 0.125, hc0, A.mult, A.add)
+            hd, hc = hdn, hcn
+        t_hk = V([t_hd], v.tensor_scalar, hdk, hd, float(NR - 1), None, A.add)
+        t_em = V([t_sm, t_st], v.tensor_tensor, encm, satm, stop, A.mult)
+        t_hx = V([t_sat, c_sm, t_hc], v.tensor_scalar, hcx, cown, sm, hc, A.mult, A.add)
+        for f in books[:2]:
+            f()
+        t_sg = V([t_em, c_rs], v.tensor_tensor_scan, seg, rst, encm, 0.0, A.mult, A.add)
+        for f in books[2:4]:
+            f()
+        t_sw = V([t_sg], v.tensor_scalar, stopw, encw, 1.0, None, A.min)
+        t_ni = V([t_sg], v.tensor_scalar, nine, encw, 9.0, None, A.is_ge)
+        if t == 0:
+            t_xp = [zeros("x1")]
+            t_cz = zeros("cc")
+            t_xp.append(zeros("x2"))
+        pa = at["fl"]
+        pre, pcol, lst = F(na), T.fl[:, pa + na - 1:pa + na], O(1)
+        mask = T.fl[:, m7a + 7 - na:m7a + 7]
+        P = BASE + QW * me
+        ac = ("ac%d" % t, nac)
+        late[t] = [ac] + ([("ah%d" % t, nah)] if nah else [])
+        t_p = V([ac, c_m7], v.tensor_tensor_scan, pre, land[:, 7 - na:7], mask, 0.0, A.add, A.mult)
+        t_ls = V([t_p, t_hx], v.tensor_scalar, lst, pcol, 0.125, hcx, A.mult, A.add)
+        t_pc = V([t_ls, t_wq, ("pre", npre)], v.tensor_copy, Zc[:, P:P + 16].bitcast(u32), T.wq[:, :].bitcast(u32).indirect(lst))
+        t_ps = S([t_ls, t_wq, ("pre", npre)], s.activation, Zs[:, P:P + 16], T.wqs[:, :].indirect(lst), AF.Copy)
+
+        def codes(via):
+            return [RemoteDMATransfer(dst_ids=[did(peers[e])], dma_engine_mask=bits(via[peers[e]]), remote_sem=T.sem["ak%d" % t],
+                                      srcs=[Zc[:, P + 4 * e:P + 4 * e + 4].bitcast(u8)], dsts=[Zc[:, P:P + 4].bitcast(u8)])
+                    for e in range(1, 4)]
+
+        def scales(via, w):
+            out = []
+            for e in range(1, 4):
+                o = 4 * e if w == 4 else 0
+                out.append(RemoteDMATransfer(dst_ids=[did(peers[e])], dma_engine_mask=bits(via[peers[e]]), remote_sem=T.sem["ap%d" % t],
+                                             srcs=[Zs[:, P + o:P + o + w]], dsts=[Zs[:, P + o - 4 * e:P + o - 4 * e + w]]))
+            return out
+
+        h = len(eon) // 2
+        if t < RD - 1:
+            need("g", [t_pc, t_ps])
+            g.remote_dma_fused(codes({side[0]: eoff[:h], side[1]: eoff[h:2 * h], mate: eon[:h]}) +
+                               scales({side[0]: eoff[2 * h:3 * h], side[1]: eoff[3 * h:], mate: eon[h:]}, 16), local_sem=T.sem.loc)
+            ncol = 3 * h
+        else:
+            via = {side[0]: eoff[:2 * h], side[1]: eoff[2 * h:], mate: eon}
+            need("g", [t_pc])
+            g.remote_dma_fused(codes(via), local_sem=T.sem.loc)
+            need("g", [t_ps])
+            g.remote_dma_fused(scales(via, 4), local_sem=T.sem.loc)
+            ncol = 6 * h
+        sent.append(2 * ncol)
+        if tail:
+            g.remote_dma_fused(tail, local_sem=T.sem.loc)
+        ends += [("ak%d" % t, ncol), ("ap%d" % t, ncol)] + late[t]
+        vi, va, vx, vo = I(4), I(4), F(4), F(4)
+        q = (F(64), F(64), F(64))
+        pl = O(4)
+        t_b = t_hk
+        if rank:
+            pr = F(1)
+            t_pr = V([], v.tensor_reduce, pr, land[:, 7 - rank:7], AxisListType.X, A.add)
+        t_wj = V([t_ni, c_jw], v.tensor_tensor, wj, nine, jw, A.add)
+        t_lg = V([t_rd], v.tensor_scalar, logo, red, 0.5, 32.0, A.mult, A.add)
+        if rank:
+            t_b = V([t_hk, t_pr], v.tensor_tensor, bcol, hdk, pr, A.add)
+        else:
+            bcol = hdk
+        t_wi = V([t_sw, c_jd], v.tensor_tensor, wid, stopw, jd, A.mult)
+        t_vi = V([t_b, t_sg], v.tensor_scalar, vi, encw, bcol, float(2 ** SH + 1), A.add, A.mult)
+        t_tw = V([t_wi, t_wj], v.tensor_tensor, tww, wid, wj, A.add)
+        t_va = V([t_vi], v.tensor_scalar, va, vi, 1, 3 * QW + 2, A.logical_shift_right, A.bitwise_and)
+        for f in books[4:5]:
+            f()
+        t_vx = V([t_va, t_sw], v.tensor_tensor, vx, va, stopw, A.mult)
+        t_vo = V([t_vx, t_tw], v.tensor_tensor, vo, vx, tww, A.add)
+        for f in books[5:]:
+            f()
+        t_pl = V([t_vo], v.tensor_copy, pl, vo)
+        if t == 0:
+            t_xp.append(zeros("x3"))
+            t_vq = V([tv], v.quantize_mx, T.vq[:, :], T.vqs[:, :], T.vt[:, :])
+        ra = 16 + 16 * t
+        t_lks = S([t_lg, t_z, t_cz], s.activation, T.ccs[:, ra:ra + 16], Zs[:, 0:128].indirect(logo), AF.Copy)
+
+        def book(bcol=bcol, t_b=t_b, q=q, t_lg=t_lg, t_z=t_z, t_st=t_st, stop=stop, sat=sat, num=num, numn=numn, ra=ra, logo=logo, Zc=Zc):
+            k = {}
+
+            def b0():
+                t_lcs.append(V([t_lg, t_z, t_cz], v.tensor_copy, T.cc[:, ra:ra + 16].bitcast(u32), Zc[:, 0:128].bitcast(u32).indirect(logo)))
+
+            def b1():
+                k[1] = V([t_b], v.tensor_scalar, q[0], sat[:, 1:65], bcol, float(NR * PL - NR), A.add, A.add)
+
+            def b2():
+                t_lis.append(V(t_num + [t_fill, t_nf], v.tensor_copy, T.sidc[:, ra:ra + 16], num[:, 0:72].indirect(logo)))
+
+            def b3():
+                k[2] = V([k[1]] + t_num, v.tensor_tensor, q[1], q[0], num[:, 0:64], A.subtract)
+
+            def b4():
+                k[3] = V([k[2], t_st], v.tensor_tensor, q[2], q[1], stop, A.mult)
+
+            def b5():
+                t_num[:] = [V([k[3]], v.tensor_tensor, numn[:, 0:64], q[2], num[:, 0:64], A.add)]
+
+            return [b0, b1, b2, b3, b4, b5]
+
+        books = book()
+        if t == RD - 2:
+            d0, n2, d1, g1, g2, l1, l2 = F(1), F(1), F(1), F(3), F(3), F(3), F(3)
+            lfin = O(3)
+            e0 = V([t_cf[1]], v.tensor_scalar, d0, counts[0], -1.0, 16.0, A.mult, A.add)
+            e1 = V([], v.tensor_tensor, n2, counts[0], counts[1], A.add)
+            e2 = V([], v.tensor_scalar, d1, counts[1], -1.0, 16.0, A.mult, A.add)
+            e4 = V([e0, c_jw], v.tensor_scalar, g1, jq, counts[0], d0, A.is_ge, A.mult)
+            e5 = V([e1, e2], v.tensor_scalar, g2, jq, n2, d1, A.is_ge, A.mult)
+            e6 = V([e4, c_j16], v.tensor_tensor, l1, g1, jq16, A.add)
+            e7 = V([e5, e6], v.tensor_tensor, l2, l1, g2, A.add)
+            t_lf = V([e7], v.tensor_copy, lfin, l2)
+        if t == RD - 1:
+            books[0]()
+            t_l2 = S([t_lks, t_lf], s.activation, T.lgs[:, :], T.ccs[:, :].indirect(lfin), AF.Copy)
+            t_l1 = V(t_lcs + [t_lf], v.tensor_copy, T.lg[:, :].bitcast(u32), T.cc[:, :].bitcast(u32).indirect(lfin))
+            dma("y", [t_l1], "st", T.oc[:, 0:192], T.lg[:, :].bitcast(u8))
+            for k in range(4):
+                dma("y", [t_l2], "st", T.osc[4 * k:4 * k + 4, 0:48], T.lgs[32 * k:32 * k + 4, :])
+        t_xc = V([t_pl, ("ak%d" % t, ncol), t_z, t_pc, t_xp[t]], v.tensor_copy, Nc[:, 0:64].bitcast(u32), Zc[:, :].bitcast(u32).indirect(pl))
+        t_xs = S([t_pl, ("ap%d" % t, ncol), t_z, t_ps, t_xp[t]], s.activation, Ns[:, 0:64], Zs[:, :].indirect(pl), AF.Copy)
+        t_X = [t_xc, t_xs]
+    t_y = run("t", t_X + [t_vq], te.matmul_mx, T.py[:, 0:128], T.vq[:, :], T.vqs[:, :], T.x3[:, :], T.x3s[:, :], True, True)
+    dma("y", [t_xc], "st", T.oc[:, 192:448], T.x3[:, 0:64].bitcast(u8))
+    for k in range(4):
+        dma("sy"[k % 2], [t_xs], "st", T.osc[4 * k:4 * k + 4, 48:112], T.x3s[32 * k:32 * k + 4, 0:64])
+    t_yc = S([t_y], s.activation, T.ys[:, :], T.py[:, 0:64], AF.Copy)
+    for f in books[1:4]:
+        f()
+    t_l3 = V(t_lis, v.tensor_copy, T.sidl[:, :], T.sidc[:, :].indirect(lfin))
+    for f in books[4:]:
+        f()
+    dma("y", [t_l3], "st", T.sid[0:1, 0:48], T.sidl[0:1, :])
+    dma("s", [t_yc], "st", T.y[:, :], T.ys[:, :])
+    dma("y", t_num, "st", T.sid[0:1, 48:112], T["num%d" % RD][0:1, 0:64])
+    need("g", list(done.items()) + list(dmas.items()) + [("loc", sum(sent)), ("pre", npre)] + ends)

@@ -2,31 +2,166 @@ from concourse.bass import DstId, RemoteDMATransfer
 from concourse.mybir import dt, AluOpType, AxisListType, ActivationFunctionType
 
 NR, PL, CS, RD = 8, 64, 16, 3
-USED = RD * CS
-BASE, SH = 144, 9
-QW = 1 << (SH - 1)
-ZW = BASE + 3 * QW + 16
+OWN, TWIN, EXTRA, XQW = 448, 192, 576, 592
+SHARE, CUT, POOR, RICH = (40, 48), (24, 32), (3, 2), (0, 3)
+WCODES = (2, 6, 6, 8)
+NCODES = (8, 8, 12)
+W4 = 112
+CODES = "float8_e4m3fn_x4"
+COMES = {"pt": 6.9, "pw": 6.9, "a1": 8.2, "b1": 8.5, "k1": 10.3, "a2": 10.5, "b2": 10.7, "px": 12.0, "k2": 13.1, "c2": 13.6,
+         "late": 16.0, "a3": 16.5, "k3": 18.5, "p3": 18.8}
+LEAVES = {"ahead": 2.2, "count1": 6.8, "cols1": 8.9, "sum1": 9.6, "count2": (9.2, 12.3), "extra": 11.0, "cols2": 11.2,
+          "late2": 14.1, "count3": 14.5, "sum2": 14.8, "cols3": 16.9, "end": 20.2}
+WAKE, ISSUE, LEAST = 0.15, 0.35, 0.09
 
 SCRATCH = {
-    "wt": ("sbuf", [128, 2048], "bfloat16"), "xt": ("sbuf", [128, 512], "bfloat16"),
-    "qt": ("sbuf", [128, 512], "bfloat16"), "ut": ("sbuf", [128, 512], "bfloat16"), "vt": ("sbuf", [128, 512], "bfloat16"),
-    "fl": ("sbuf", [128, 3000], "float32"), "il": ("sbuf", [128, 256], "int32"), "ol": ("sbuf", [128, 128], "uint16"),
-    "sidc": ("sbuf", [128, 96], "float32"), "sidl": ("sbuf", [128, 48], "float32"), "ys": ("sbuf", [128, 64], "float32"),
+    "wt": ("sbuf", [128, 2048], "bfloat16"), "xt": ("sbuf", [128, 1024], "bfloat16"),
+    "ut": ("sbuf", [128, 512], "bfloat16"), "vt": ("sbuf", [128, 512], "bfloat16"),
+    "fl": ("sbuf", [128, 3600], "float32"), "il": ("sbuf", [128, 256], "int32"), "ol": ("sbuf", [128, 128], "uint16"),
+    "bl": ("sbuf", [128, 1280], "bfloat16"), "ys": ("sbuf", [128, 64], "float32"), "num": ("sbuf", [128, 128], "float32"),
     "ha": ("psum", [128, 512], "float32"), "py": ("psum", [128, 512], "float32"),
 }
-for _n, _w in (("wc", 512), ("uq", 128), ("ua", 128), ("ub", 128), ("vq", 128), ("wq", 256), ("cc", 128), ("lg", 48),
-               ("x0", 128), ("x1", 128), ("x2", 128), ("x3", 128), ("z0", ZW), ("z1", ZW), ("z2", ZW)):
-    SCRATCH[_n] = ("sbuf", [128, _w], "float8_e4m3fn_x4")
+for _n, _w in (("wc", 512), ("uq", 128), ("ua", 128), ("ub", 128), ("vq", 128), ("xq", XQW), ("cc", 128), ("fin", 176),
+               ("x1", 128), ("x2", 192), ("x3", 160), ("x4", 192), ("z2", 128), ("z3", 128)):
+    SCRATCH[_n] = ("sbuf", [128, _w], CODES)
     SCRATCH[_n + "s"] = ("sbuf", [128, _w], "uint8")
-for _t in range(RD):
+for _t in range(1, RD + 1):
     SCRATCH["at%d" % _t] = ("sbuf", [128, 512], "bfloat16")
-    SCRATCH["sat%d" % _t] = ("sbuf", [128, 72], "bfloat16")
-    SCRATCH["cnt%d" % _t] = ("sbuf", [128, 8], "bfloat16")
-for _t in range(RD + 1):
-    SCRATCH["num%d" % _t] = ("sbuf", [128, 72], "float32")
+    SCRATCH["cnt%d" % _t] = ("sbuf", [128, 16], "bfloat16")
+    SCRATCH["out%d" % _t] = ("sbuf", [128, 144], "bfloat16")
+for _t in range(4):
     SCRATCH["pz%d" % _t] = ("psum", [128, 512], "float32")
-SEMAPHORES = ["vs", "ss", "ts", "gs", "lqx", "lu", "lx", "lv", "lw0", "lw1", "st", "pre", "loc"]
-SEMAPHORES += [k + str(t) for k in ("ac", "ah", "ak", "ap") for t in range(RD)]
+SEMAPHORES = ["vs", "ss", "ts", "gs", "lqx", "lu", "lx", "lv", "lw0", "lw1", "st", "loc",
+              "pw", "pt", "px", "a1", "a2", "a3", "b1", "b2", "c2", "k1", "k2", "k3", "p3"]
+
+
+def plan(r, cores, topo):
+    core = cores[r]
+
+    def quad_of(i):
+        return [j for j, d in enumerate(cores) if d in topo.cores_of(cores[i]) or topo.mates(cores[i], d)]
+
+    quad = quad_of(r)
+    first = quad_of(0)
+    second = [j for j in range(NR) if j not in first]
+    me, half = quad.index(r), 0 if r in first else 1
+    twin = [j for j in range(NR) if j not in quad and topo.same_plane(core, cores[j]) and topo.die(cores[j]) == topo.die(core)][0]
+    mate = [j for j in quad if j != r and cores[j] in topo.cores_of(core)][0]
+    eoff = topo.engines(core, cores[twin])
+    eon = [e for e in topo.engines(core, cores[mate]) if e not in eoff][::2]
+
+    def call(writes):
+        out = []
+        for es, ws in ((eoff, [w for w in writes if w[0] != mate]), (eon, [w for w in writes if w[0] == mate])):
+            groups = []
+            for w in ws:
+                same = [x for x in groups if x[0] == w[1:3]]
+                if same:
+                    same[0][1].append((w[0], w[3]))
+                else:
+                    groups.append((w[1:3], [(w[0], w[3])]))
+            if len(groups) > 1 and len(ws) in (2, 4):
+                groups = [(w[1:3], [(w[0], w[3])]) for w in ws]
+            groups.sort(key=lambda x: -len(x[1]))
+            n = len(es)
+            cuts = {0: [], 1: [n], 2: [n // 2] * 2, 3: [n // 2, n // 4, n // 4], 4: [n // 4] * 4}[len(groups)]
+            a = 0
+            for (key, ds), c in zip(groups, cuts):
+                out.append((es[a:a + c], key[0], key[1], ds))
+                a += c
+        return out
+
+    def both(buf, d, sem, a, b, nc, ns, sems=None):
+        return [(4 * nc, (d, sem, (buf, a, nc), (buf, b, nc))), (ns, (d, sems or sem, (buf + "s", a, ns), (buf + "s", b, ns)))]
+
+    def calls(ws, order=None):
+        wide = []
+        for n, w in ws:
+            if n not in wide:
+                wide.append(n)
+        return [call([w for n, w in ws if n == k]) for k in (sorted(wide, reverse=True) if order else wide)]
+
+    P = {}
+    ws = []
+    for a in reversed(first):
+        if a not in (r, twin):
+            ws += both("xq", a, "pw", OWN, 64 * ((r - a - 1) % NR), WCODES[first.index(a)], 8)
+    poor = me == POOR[1 - half]
+    n = CUT[1 - half] if poor else SHARE[1 - half]
+    tw = both("xq", twin, "pt", OWN, TWIN, n, n)
+    P["ahead"] = calls(tw + ws if half else ws + tw)
+    rich = quad_of(twin)[RICH[1 - half]]
+    P["extra"] = calls(both("xq", rich, "px", OWN + n, EXTRA, 16, 16)) if poor else []
+
+    def slot(d, s):
+        others = [j for j in range(NR - 1, -1, -1) if j != d and (d in second or j in first)]
+        return (1 if d in second else 4) + others.index(s)
+
+    for t in (1, 2, 3):
+        if half:
+            ds = [d for d in reversed(quad) if d != r] if t < 3 or me < 3 else []
+        else:
+            up, down = [d for d in reversed(quad) if d > r], [d for d in quad if d < r]
+            far = second[3:] + second[:3] if t < 3 else second
+            ds = up + far + down if t == 1 else far + (up + down if t < 3 or me < 3 else [])
+        sem = "c2" if half and t == 2 else "a%d" % t
+        src = ("out%d" % t, 63 if t == 1 else 127, 1)
+        ws = [(d, "b%d" % t if d < r and not half and (t == 1 or me == 3) else sem, src, ("cnt%d" % t, slot(d, r), 1)) for d in ds]
+        now = [w for w in ws if w[1] == sem or w[0] == mate]
+        P["count%d" % t] = [call(x) for x in (now, [w for w in ws if w not in now]) if x]
+        if half and t < 3:
+            P["sum%d" % t] = [call([(twin, "a%d" % (t + 1), ("out%d" % t, 130, 1), ("cnt%d" % (t + 1), 7, 1))])]
+    peers = [quad[(me + e) % 4] for e in range(4)]
+
+    def plain(buf, base, sem, sems=None):
+        ws = []
+        for e in range(1, 4):
+            ws += both(buf, peers[e], sem, base + 16 * me + 4 * e, base + 16 * me, 4, 4, sems)
+        return calls(ws)
+
+    P["cols1"] = plain("x2", 0, "k1") if half else []
+    if half:
+        ws = []
+        for j in (2, 1, 0):
+            if j != me:
+                ws += both("x3", quad[j], "k2", 16 * me if me < 3 else 144, 16 * me, NCODES[j], 12)
+        P["cols2"] = calls(ws, True)
+        P["late2"] = calls(both("x3", quad[3], "k2", 144 + 4 * (3 - me), 16 * me, 4, 4)) if me < 3 else []
+    else:
+        P["cols2"] = plain("x3", 0, "k2")
+    if me == RICH[half]:
+        order = [1, 2, 3, 0] if me == 0 else [3, 0, 1, 2]
+        base = W4 + 16 * me - 8 * order.index(me)
+        ws = []
+        for e, j in enumerate(order):
+            if j != me:
+                ws += both("x4", quad[j], "k3", base + 8 * e, W4 + 16 * me, 6, 6, "p3")
+        P["cols3"] = calls(ws)
+    else:
+        P["cols3"] = plain("x4", W4, "k3", "p3")
+    return P, quad, twin
+
+
+def arrange(N):
+    for n in reversed(N):
+        for d in n["deps"]:
+            N[d]["last"] = min(N[d]["last"], n["last"] - WAKE - N[d]["lat"])
+    free, order, left = {}, [], [len(n["deps"]) for n in N]
+    ready = [i for i, n in enumerate(N) if not left[i]]
+    while ready:
+        est = {i: max([free.get(N[i]["q"], 0.0), N[i]["from"]] +
+                      [N[d]["end"] + (0.0 if N[d]["q"] == N[i]["q"] == "t" or N[d]["kind"] == "r" else WAKE) for d in N[i]["deps"]]) for i in ready}
+        a = min(ready, key=lambda i: est[i] + N[i]["dur"])
+        i = min([j for j in ready if N[j]["q"] == N[a]["q"] and est[j] < est[a] + N[a]["dur"]], key=lambda j: (N[j]["last"], j))
+        free[N[i]["q"]] = est[i] + N[i]["dur"]
+        N[i]["end"] = est[i] + N[i]["lat"]
+        order.append(i)
+        ready.remove(i)
+        for j in N[i]["next"]:
+            left[j] -= 1
+            if not left[j]:
+                ready.append(j)
+    return order
 
 
 def rank_program(g, core, T, topo):
@@ -36,43 +171,501 @@ def rank_program(g, core, T, topo):
     A, AF = AluOpType, ActivationFunctionType
     v, s, te, sy = g.vector, g.scalar, g.tensor, g.sync
     u8, u32 = dt.uint8, dt.uint32
+    plans = [plan(r, T.cores, topo) for r in range(NR)]
+    P, quad, twin = plans[rank]
+    me, half = quad.index(rank), 1 if twin < rank else 0
+    rich, poor = me == RICH[half], me == POOR[half]
+    late = half == 1 and me == 3
+    comes = {}
+    for p in plans:
+        for cs in p[0].values():
+            for c in cs:
+                for es, sem, src, ds in c:
+                    for d, dst in ds:
+                        if d == rank:
+                            comes[sem] = comes.get(sem, 0) + len(es)
 
-    def quad_of(c):
-        return [d for d in T.cores if d in topo.cores_of(c) or topo.mates(c, d)]
+    N, seen_by, sent = [], {}, [0]
 
-    quad = quad_of(core)
-    me = quad.index(core)
-    mate = [d for d in quad if d in topo.cores_of(core) and d != core][0]
-    side = [d for d in quad if d not in topo.cores_of(core)]
-    other = [d for d in T.cores if d not in quad]
-    twin = [d for d in other if topo.same_plane(core, d) and topo.die(d) == topo.die(core)][0]
-    half = 0 if rank < T.rank_of(twin) else 1
-    r0 = T.rank_of(quad[0])
-    peers = [quad[(me + e) % 4] for e in range(4)]
-    eoff = topo.engines(core, side[0])
-    eon = [e for e in topo.engines(core, mate) if e not in eoff][::2]
+    def R(name, a, b, st=1):
+        ap = T[name][:, a:b:st] if st > 1 else T[name][:, a:b]
+        psum = SCRATCH[name][0] == "psum"
+        return (ap, name, 0 if psum else a, 512 if psum else b, len(range(a, b, st)), None)
 
-    def urgent(sr, d):
-        return sr < max(T.rank_of(c) for c in quad_of(d))
+    def words(name, a, b):
+        return (T[name][:, a:b].bitcast(u32), name, a, b, b - a, None)
 
-    def wanted(sr, d, t):
-        return t < RD - 1 or urgent(sr, d)
+    def by(w, off):
+        return (w[0].indirect(off[0]), w[1], w[2], w[3], 16 * off[4], off)
 
-    def early(sr, d):
-        return urgent(sr, d) or T.cores[sr] in quad_of(d)
+    def note(q, kind, fn, outs, ins, dur, lat=None, ext=(), after=(), last=99.0, sem=None):
+        i = len(N)
+        deps = set(after)
+        ins = ins + [x[5] for x in outs + ins if x[5]]
+        for x, w in [(x, False) for x in ins] + [(x, True) for x in outs]:
+            for j, a, b, jw in seen_by.setdefault(x[1], []):
+                if (w or jw) and a < x[3] and x[2] < b and j != i:
+                    deps.add(j)
+            seen_by[x[1]].append((i, x[2], x[3], w))
+        ext = [e for e in ext if e in comes]
+        N.append({"q": q, "kind": kind, "fn": fn, "deps": sorted(deps), "next": [], "dur": dur, "lat": lat or dur, "ext": ext, "sem": sem,
+                  "from": max([0.0] + [COMES["late" if late and e == "k2" else e] for e in ext]), "last": last})
+        for d in deps:
+            N[d]["next"].append(i)
+        return i
 
-    def bits(es):
-        return sum(1 << e for e in es)
+    def op(q, call, *a, outs=1, ext=(), after=(), dur=None, both=False, **k):
+        views = [x for x in a if isinstance(x, tuple)]
+        o = views[:outs] + [k[x] for x in k if x == "accum_out"]
+        i = views[outs:] + [k[x] for x in k if x != "accum_out" and isinstance(k[x], tuple)]
+        if dur is None:
+            n = views[0][4]
+            if views[0][5]:
+                dur = 0.05 + 0.003 * n
+            elif [x for x in i if x[5]]:
+                dur = 0.06 + 0.0015 * n
+            else:
+                dur = max(LEAST, 0.001 * max(x[4] for x in views) * (2 if both else 1))
+        a2 = [x[0] if isinstance(x, tuple) else x for x in a]
+        k2 = {x: k[x][0] if isinstance(k[x], tuple) else k[x] for x in k}
+        return note(q, "c", lambda: call(*a2, **k2), o, i, dur, ext=ext, after=after)
 
-    def did(d):
-        rid, pid = topo.addr(d, core)
-        return DstId(rid=rid, pnc=pid)
+    def V(call, *a, **k):
+        return op("v", call, *a, **k)
+
+    def S(out, in_, f, **k):
+        return op("s", s.activation, out, in_, f, **k)
+
+    def ts(out, a, s1, s2, o0, o1=None, **k):
+        return V(v.tensor_scalar, out, a, s1, None, o0, **k) if o1 is None else V(v.tensor_scalar, out, a, s1, s2, o0, o1, **k)
+
+    def quant(dst, a, n, src, b):
+        return V(v.quantize_mx, R(dst, a, a + n), R(dst + "s", a, a + n), R(src, b, b + 4 * n), outs=2, dur=0.012 + 0.00088 * n)
+
+    def mm(out, w, a, x, b, start, stop, **k):
+        return op("t", te.matmul_mx, R(out, 0, 128), R(w, a, a + 128), R(w + "s", a, a + 128), R(x, b, b + 128), R(x + "s", b, b + 128),
+                  start, stop, dur=0.09, **k)
+
+    def iota(out, pattern, base, cm=0):
+        k = {} if out[1] == "il" else {"allow_small_or_imprecise_dtypes": True}
+        return op("g", g.iota, out, pattern, base, cm, dur=0.13 + 0.002 * out[4], **k)
+
+    def load(q, sem, dst, src, lat, last, **k):
+        return note(q, "d", lambda: (s if q == "s" else sy).dma_start(dst[0], src), [dst], [], 0.05, lat, sem=sem, last=last, **k)
+
+    def store(q, dst, src, reads):
+        return note(q, "d", lambda: (s if q == "s" else sy).dma_start(dst, src), [], [reads], 0.05, sem="st", last=LEAVES["end"])
+
+    def send(name, after=()):
+        last = LEAVES[name][half] if isinstance(LEAVES[name], tuple) else LEAVES[name]
+        for m, c in enumerate(P.get(name, [])):
+            def raw(x):
+                a = T[x[0]][:, x[1]:x[1] + x[2]]
+                return a.bitcast(u8) if SCRATCH[x[0]][2] == CODES else a
+            trs = []
+            for es, sem, src, ds in c:
+                ids = [topo.addr(T.cores[d], core) for d, dst in ds]
+                trs.append(RemoteDMATransfer(dst_ids=[DstId(rid=a, pnc=b) for a, b in ids], dma_engine_mask=sum(1 << e for e in es),
+                                             remote_sem=T.sem[sem], srcs=[raw(src)], dsts=[raw(dst) for d, dst in ds]))
+                sent[0] += len(es)
+            note("g", "r", lambda trs=trs: g.remote_dma_fused(trs, local_sem=T.sem.loc), [],
+                 [R(x[2][0], x[2][1], x[2][1] + x[2][2]) for x in c], ISSUE, after=after, last=last + ISSUE * m)
+
+    at = {"fl": 0, "il": 0, "ol": 0, "bl": 0}
+
+    def take(buf, n):
+        al = {"fl": 8, "il": 1, "ol": 2, "bl": 16}[buf] if n > 1 or buf == "ol" else 1
+        a0 = -(-at[buf] // al) * al
+        at[buf] = a0 + n
+        return lambda a=0, b=n, st=1: R(buf, a0 + a, a0 + b, st)
+
+    def F(n=1):
+        return take("fl", n) if n > 1 else take("fl", 1)()
+
+    def I(n=1):
+        return take("il", n)()
+
+    def O(n=1):
+        return take("ol", n)
+
+    def pick(dst, a, n, src, lo, hi, lst, ext=(), exts=None):
+        V(v.tensor_copy, words(dst, a, a + n), by(words(src, lo, hi), lst), ext=ext)
+        S(R(dst + "s", a, a + n), by(R(src + "s", lo, hi), lst), AF.Copy, ext=exts or ext)
+
+    load("s", "lu", R("ut", 0, 8), T.u[:, 0:8], 1.6, -5.0)
+    load("y", "lqx", R("xt", 256, 448), T.qx[:, 0:192], 1.9, -5.0)
+    load("s", "lw0", R("wt", 0, 1536), T.w[:, 0:1536], 3.7, -4.0)
+    load("y", "lx", R("xt", 0, 256), T.x[:, :], 3.9, -4.0)
+    load("y", "lw1", R("wt", 1536, 2048), T.w[:, 1536:2048], 4.5, -3.0)
+
+    ip, ip2, neg, rs0, row, jw0 = I(), I(), F(3), F(64), F(80), F(3)
+    iota(ip, [[0, 1]], 0, 1)
+    iota(ip2, [[0, 1]], 4 * me, 1)
+    iota(rs0(), [[0, 4], [1, 16]], 0)
+    if me < 3:
+        iota(neg(0, 3 - me), [[1, 3 - me]], -3)
+    if me > 0:
+        iota(neg(3 - me, 3), [[1, me]], 1 - me)
+    iota(row(), [[1, 80]], 0)
+    iota(jw0(), [[16, 3]], 0)
+    krow = rs0(0, 16)
+    V(v.memset, R("xt", 448, 1024), 0.0, dur=0.3)
+    lua, lub, lw = O(8), O(8), {1: O(5), 2: O(5), 3: O(4)}
+    V(v.memset, lua(), 0)
+    V(v.memset, lub(), 2)
+    c16, mk, seed, zero = take("bl", 128), F(9), F(16), F(64)
+    V(v.memset, seed(), 2.0 ** 60)
+    fills = [quant("x2", 0, 128, "xt", 448), quant("x4", 0, 128, "xt", 448), quant("x3", 0, 144, "xt", 256)]
+    quant("cc", 0, 128, "xt", 448)
+    quant("fin", 48, 128, "xt", 256)
+    ik, kcol, kcol2, ic, dcol, ih, isl, b3, hc0a, hc0, sm, m16 = I(), F(), F(), I(), F(), I(), I(), I(), F(), F(), F(), F(64)
+    ts(ik, ip, 15, None, A.bitwise_and)
+    ts(ic, ip2, 2, 3, A.logical_shift_right, A.bitwise_and)
+    ts(ih, ip, 1, 1, A.logical_shift_right, A.bitwise_and)
+    ts(isl, ip, 1, None, A.bitwise_and)
+    ts(b3, ip, 3, 1, A.logical_shift_right, A.bitwise_and)
+    V(v.tensor_copy, kcol, ik)
+    V(v.tensor_copy, dcol, ic)
+    ts(kcol2, b3, 400.0, kcol, A.mult, A.add)
+    loc = (TWIN, OWN) if half else (OWN, TWIN)
+    ts(hc0a, ih, loc[1] - loc[0] - 0.5, loc[0] + (3.5 - me) / 8.0, A.mult, A.add)
+    c0 = 1 if half else 4
+    V(v.memset, mk(0, 8), 1.0)
+    V(v.memset, mk(8, 9), 0.125)
+    ts(sm, dcol, float(me), 0.125, A.is_gt, A.mult)
+    ts(mk(c0, c0 + 3), neg(), dcol, 0.0, A.add, A.is_gt)
+    ts(hc0, isl, hc0a, None, A.add)
+    ts(m16(), rs0(), kcol, None, A.is_equal)
+    for t in (1, 2):
+        V(v.memset, lw[t](4, 5), 128)
+    want = {t: take("bl", 144) for t in (1, 2, 3)}
+    S(R("ut", 12, 512), R("xt", 448, 948), AF.Copy)
+    S(R("at1", 256, 512), R("xt", 448, 704), AF.Copy)
+    big, rst, kh, hbig, nbig, k512, jw = F(16), F(64), F(), F(), F(), F(16), F(3)
+    S(big(), seed(), AF.Square)
+    S(rst(), rs0(), AF.Sign)
+    S(kh, kcol, AF.Copy, bias=0.5)
+    S(hbig, big(0, 1), AF.Copy, scale=0.5)
+    S(nbig, big(0, 1), AF.Copy, scale=-0.5)
+    S(k512(), krow, AF.Copy, bias=float(NR * PL))
+    S(jw(), jw0(), AF.Identity, bias=kcol)
+
+    def num(a=0, b=80):
+        return R("num", 48 + a, 48 + b)
+
+    sidc, lrow, thr = F(80), {t: F(80) for t in (1, 2, 3)}, {2: F(144), 3: F(144)}
+    S(num(0, 64), row(0, 64), AF.Copy, bias=float(PL * rank))
+    S(num(64, 80), row(0, 16), AF.Copy, bias=-1.0, scale=0.0)
+    S(sidc(48, 80), row(0, 32), AF.Copy, bias=-1.0, scale=0.0)
+    S(zero(), row(0, 64), AF.Copy, scale=0.0)
+    wide = {2: not half, 3: half and not late}
+    for t in (2, 3):
+        if wide[t]:
+            S(thr[t](64, 144), row(), AF.Copy, scale=0.0)
+        elif not (late and t == 3):
+            for a in (0, 64):
+                S(thr[t](a, a + 64), row(0, 64), AF.Identity, scale=0.0, bias=big(0, 1))
+    for t in (1, 2, 3):
+        S(R("cnt%d" % t, 8, 9), row(0, 1), AF.Copy)
+        S(want[t](64, 80) if t == 1 else want[t](128, 144), row(0, 16), AF.Copy, bias=1.0, scale=0.0)
+        S(lrow[t](), row(), AF.Copy, bias=64.0 if t < 3 else 0.0)
+    S(c16(), R("xt", 448, 576), AF.Copy, bias=16.0)
+    hp = POOR[half] + 4 * (1 - half)
+    pt, n8 = F(800), 8 * SHARE[half]
+
+    quant("xq", OWN, 128, "xt", 256)
+    send("ahead")
+    S(R("ut", 8, 12), R("ut", 4, 8), AF.Copy, scale=-1.0)
+    quant("uq", 0, 128, "ut", 0)
+    pick("ub", 0, 128, "uq", 0, 128, lub())
+    pick("ua", 0, 128, "uq", 0, 128, lua())
+    quant("x1", 0, 128, "xt", 0)
+    for i in range(4):
+        quant("wc", 128 * i, 128, "wt", 512 * i)
+
+    sat = {t: take("bl", 80) for t in (2, 3)}
+    sat[1] = lambda: R("out1", 0, 80)
+    cown = {t: R("out%d" % t, 63 if t == 1 else 127, 64 if t == 1 else 128) for t in (1, 2, 3)}
+    logo = {t: O() for t in (1, 2, 3)}
+    hd, hc = {}, {1: hc0}
+
+    def land(t, a, b):
+        return R("cnt%d" % t, a, b)
+
+    def layer(t, ext=()):
+        n = 64 if t == 1 else 128
+        for i in range(4):
+            mm("pz%d" % i, "wc", 128 * i, "x%d" % t, 0, True, True, ext=ext)
+        for i in range(4):
+            o, z = R("at%d" % t, i, 4 * n, 4), R("pz%d" % i, 0, n)
+            o = o[:1] + ("at%d.%d" % (t, i),) + o[2:]
+            if i % 2:
+                ts(o, z, 0.0, 0.0625, A.max, A.mult)
+            else:
+                S(o, z, AF.Relu, scale=0.0625)
+        dst, a = ("x2", 64) if t == 1 else ("z%d" % t, 0)
+        j = len(N)
+        V(v.quantize_mx, R(dst, a, a + 128), R(dst + "s", a, a + 128), R("at%d" % t, 0, 512), outs=2, dur=0.125, after=range(j - 4, j))
+        mm("ha", "ua", 0, dst, a, True, False)
+        mm("ha", "ub", 0, dst, a, False, True)
+
+    def count(t):
+        if t == 1:
+            ts(want[1](0, 64), R("ha", 0, 64), 0.0, None, A.is_gt)
+            V(v.tensor_tensor_scan, sat[1](), want[1](0, 80), c16(0, 80), 0.0, A.add, A.min)
+        elif late and t == 3:
+            ts(want[t](0, 128), R("ha", 0, 128), 0.0, None, A.is_gt)
+        else:
+            V(v.tensor_tensor, want[t](0, 128), R("ha", 0, 128), thr[t](0, 128), A.is_gt)
+            V(v.tensor_tensor_scan, R("out%d" % t, 0, 128), want[t](0, 128), c16(), 0.0, A.add, A.min, dur=LEAST)
+
+    def stops(t):
+        wg, red = take("bl", 80), F()
+        if t > 1:
+            S(wg(), by(want[t](0, 144), lw[t - 1]()), AF.Copy)
+            V(v.tensor_tensor_scan, sat[t](), wg(), c16(0, 80), 0.0, A.add, A.min)
+        S(F(80)(), sat[t](), AF.Sign, bias=kh, scale=-1.0, accum_out=red)
+        ts(logo[t](), red, 0.5, 40.0, A.mult, A.add)
+
+    def add_up(t, a, b, ext):
+        o = F()
+        S(F(8)(0, b - a), land(t, a, b), AF.Identity, accum_out=o, ext=ext)
+        return o
+
+    def head(t):
+        hd[t], hc[t], o = F(), F(), F()
+        tot = add_up(t - 1, c0, 7 if t == 2 and not half else 8, ["a%d" % (t - 1), "b%d" % (t - 1)] + (["c2"] if t == 3 else []))
+        if t == 2:
+            S(hd[t], tot, AF.Identity, bias=cown[1])
+        else:
+            S(o, cown[2], AF.Identity, bias=hd[2])
+            S(hd[t], tot, AF.Identity, bias=o)
+        S(hc[t], hd[t], AF.Identity, scale=0.125, bias=hcr if rich and t == 3 else hc0)
+
+    def mine(t, m=sm):
+        o = F()
+        S(o, cown[t], AF.Identity, scale=m, bias=hc[t])
+        return o
+
+    def serve(t, ext, lo, dst, a, h, clip=None):
+        pre, lst = F(9), O()
+        V(v.tensor_tensor_scan, pre(lo, 9), land(t, lo, 9), mk(lo, 9), 0.0, A.add, A.mult, ext=ext)
+        if clip is None:
+            ts(lst(), pre(8, 9), h, None, A.add)
+        else:
+            ts(lst(), pre(8, 9), h, clip, A.add, A.min)
+        pick(dst, a, 16, "xq", 0, EXTRA, lst(), ["pt", "pw"])
+
+    def refills(t, ext, o=None):
+        lp, l2, mrow, posk, nk, st = O(), O(), F(16), F(16), F(16), F()
+        pr = add_up(t, c0 + 3 - me, 8, ext)
+        k = kcol2 if o is None else kcol
+        if t == 1:
+            ts(lp(), k, pr, None, A.add)
+            st = pr
+        else:
+            ts(lp(), k, pr, hd[t], A.add, A.add)
+            S(st, pr, AF.Identity, bias=hd[t])
+        if o is None:
+            S(posk(), by(pt(), lp()), AF.Copy, bias=float(W4 if t == 3 else 0))
+        else:
+            ts(l2(), kcol, o, None, A.add, ext=ext)
+            S(mrow(), by(mt(), l2()), AF.Copy)
+            V(v.tensor_tensor, posk(), by(pt(), lp()), mrow(), A.add)
+        S(nk(), k512(), AF.Identity, bias=st)
+        return posk, nk
+
+    def places(t, posk):
+        lm, sg = F(64), F(64)
+        V(v.tensor_copy, by(lrow[t](), logo[t]()), posk())
+        V(v.tensor_tensor, lm(), lrow[t](0, 64), m16(), A.mult, both=True)
+        V(v.tensor_tensor_scan, sg(), rst(), lm(), 0.0, A.mult, A.add)
+        V(v.tensor_copy, lw[t](0, 4), sg(15, 64, 16))
+
+    def gate(t):
+        V(v.tensor_copy, by(thr[t](0, 128), lw[t - 1](0, 4)), zero())
+
+    def order(t):
+        pick("x%d" % (t + 1), 64 if t < 3 else 0, 64, "z%d" % t, 0, 128, lw[t - 1](0, 4))
+
+    def book(t, nk):
+        s0 = 64 if t < 3 else 0
+        pick("cc", 16 * t - 16, 16, "x%d" % (t + 1), s0, s0 + 80, logo[t]())
+        S(sidc(16 * t - 16, 16 * t), by(num(), logo[t]()), AF.Copy)
+        V(v.tensor_copy, by(num(), logo[t]()), nk())
+        if t < 3:
+            S(num(64, 80), row(0, 16), AF.Copy, bias=-1.0, scale=0.0)
+
+    def window(t, kx, shift, sem):
+        hn, hb, kp, dd, o = F(), F(), F(64), F(64), F()
+        V(v.tensor_copy, by(thr[t](64, 144), logo[t - 1]()), big())
+        S(hn, cown[t - 1], AF.Copy, scale=-0.5, bias=0.5 - shift)
+        S(hb, cown[t - 1], AF.Identity, scale=nbig, bias=hbig)
+        S(kp(), kx, AF.Identity, bias=hn)
+        if me == 0:
+            o = 0.0
+        elif me == 1:
+            o = land(t - 1, c0 + 2, c0 + 3)
+        elif me == 2:
+            S(o, land(t - 1, c0 + 1, c0 + 2), AF.Identity, bias=land(t - 1, c0 + 2, c0 + 3), ext=[sem])
+        else:
+            o = add_up(t - 1, c0, c0 + 3, [sem])
+        S(dd(), kp(), AF.Abs, scale=-1.0, bias=o, ext=[sem] if me else [])
+        S(thr[t](0, 64), dd(), AF.Relu, scale=big(0, 1), bias=hb)
+        return o
+
+    def total(t, sem):
+        S(R("out%d" % t, 130, 131), add_up(t, 1, 4, [sem]), AF.Identity, bias=cown[t])
+        send("sum%d" % t)
+
+    clip, hcr, mkr, smr = F(), F(), [F(9), F(9)], [F(), F()]
+    if poor:
+        top = TWIN + CUT[half] - 1.0
+        ts(clip, ih, (top - 4095.0) * (-1 if half else 1), top if half else 4095.0, A.mult, A.add)
+    if rich:
+        turn = [1, 2, 3, 0] if me == 0 else [3, 0, 1, 2]
+        i3, t1, t2, t3 = I(), F(), F(), F()
+        v0, v1, v2 = loc[0] + (3.5 - me) / 8.0, loc[1] + (3.5 - me - 4) / 8.0, EXTRA - CUT[half] + (3.5 - hp) / 8.0
+        ts(i3, ip, 1, 3, A.logical_shift_right, A.bitwise_and)
+        for c in (0, 1):
+            d = F()
+            S(mkr[c](), mk(), AF.Copy)
+            ts(d, b3, float(turn[2 * c + 1] - turn[2 * c]), float(turn[2 * c]), A.mult, A.add)
+            ts(mkr[c](c0, c0 + 3), neg(), d, 0.0, A.add, A.is_gt)
+            if not late:
+                ts(smr[c], d, float(me), 0.125, A.is_gt, A.mult)
+        ts(t1, i3, 1.0, v1 - v0, A.is_equal, A.mult)
+        ts(t2, i3, 2.0, v2 - v0, A.is_equal, A.mult)
+        ts(clip, i3, 2.0, float(EXTRA), A.is_equal, A.mult)
+        ts(t3, isl, t1, t2, A.add, A.add)
+        S(hcr, t3, AF.Copy, bias=v0)
+
+    layer(1)
+    count(1)
+    send("count1", fills)
+    iota(pt(0, n8), [[0, n8 // 8], [2, 2], [16, 4]], 0)
+    V(v.memset, pt(8 * CUT[half] + hp, n8, 8), 16.0 * RICH[half] + 4)
+    S(pt(400, 400 + n8), pt(0, n8), AF.Copy, bias=1.0)
+    stops(1)
+    if not half:
+        ipw, two, wa, wc0, wc1, lwin, posk, nk = I(), F(4), I(), F(), F(), O(4), F(16), F(16)
+        iota(ipw, [[0, 1]], NR - 1 - me, 1)
+        iota(two(), [[2, 4]], 0)
+        ts(wa, ipw, 7, None, A.bitwise_and)
+        ts(wc0, wa, 64.0, None, A.mult)
+        ts(wc1, b3, wc0, None, A.add)
+        ts(lwin(), two(), wc1, None, A.add)
+        w0 = 48 - 16 * me
+        pick("x2", w0, 64 - w0, "xq", 0, EXTRA, lwin(0, me + 1), ["pt", "pw"])
+        o = window(2, row(0, 64), float(w0), "a1")
+        layer(2)
+        count(2)
+        send("count2")
+        send("extra")
+        kw = F(16)
+        S(kw(), krow, AF.Copy, bias=float(w0))
+        S(posk(), kw(), AF.Identity, bias=o, ext=["a1"] if me else [])
+        S(nk(), k512(), AF.Identity, bias=o, ext=["a1"] if me else [])
+        places(1, posk)
+        book(1, nk)
+        head(2)
+        order(2)
+        stops(2)
+        serve(2, ["a2"], c0 if me == 3 else c0 + 1, "x3", 16 * me, mine(2))
+        send("cols2")
+        posk, nk = refills(2, ["a2"])
+        places(2, posk)
+        gate(3)
+        layer(3, ["k2"])
+        count(3)
+        send("count3")
+    else:
+        e4, hcn, hcn2 = I(), F(), F()
+        ts(e4, ip, 2, 3, A.logical_shift_right, A.bitwise_and)
+        ts(hcn, e4, 2.0, hc0, A.mult, A.add)
+        serve(1, ["a1"], c0, "x2", 16 * me, mine(1))
+        send("cols1")
+        total(1, "a1")
+        send("extra")
+        posk, nk = refills(1, ["a1"])
+        places(1, posk)
+        book(1, nk)
+        head(2)
+        gate(2)
+        S(hcn2, hd[2], AF.Identity, scale=0.125, bias=hcn)
+        serve(2, ["a2"], 4, "x3", 144 if late else 16 * me, hcn2)
+        send("cols2")
+        layer(2, ["k1"])
+        order(2)
+        count(2)
+        send("count2")
+        stops(2)
+        serve(2, ["a2", "c2"], c0, "x3", 48 if late else 144, mine(2))
+        send("late2")
+        if not late:
+            hm, m8, mt, ki, kj, kx = F(64), F(64), F(64), I(64), I(64), F(64)
+            for b in (0, 1):
+                iota(hm(b, 64, 2), [[1, 4], [0, 4], [4, 2]], 512)
+                iota(m8(b, 64, 2), [[0, 4], [16, 4], [0, 2]], 8 * b)
+            if me:
+                iota(mt(), [[4, 4], [1, 2], [0, 8]], 0)
+            ts(ki, hm(), add_up(2, 4, 8, ["a2"]), hd[2], A.subtract, A.subtract)
+            ts(kj, ki, 7, None, A.bitwise_and)
+            V(v.tensor_tensor, kx(), kj, m8(), A.add, both=True)
+            o = window(3, kx(), 0.0, "c2")
+            layer(3, ["k2"])
+            count(3)
+            send("count3")
+            posk, nk = refills(2, ["a2", "c2"] if me else ["a2"], o if me else None)
+            places(2, posk)
+        else:
+            posk, nk = refills(2, ["a2", "c2"])
+            places(2, posk)
+            layer(3, ["k2"])
+            count(3)
+        total(2, "c2")
+    load("y", "lv", R("vt", 0, 512), T.v[:, :], 2.1, 99.0, ext=["c2" if late else "k2"])
+    quant("vq", 0, 128, "vt", 0)
+    book(2, nk)
+    order(3)
+    stops(3)
+    head(3)
+    lo = c0 if me == 3 else c0 + 1
+    if rich:
+        pre, lst = [F(9), F(9)], O(2)
+        for c in (0, 1):
+            V(v.tensor_tensor_scan, pre[c](lo, 9), land(3, lo, 9), mkr[c](lo, 9), 0.0, A.add, A.mult, ext=["a3"])
+            ts(lst(c, c + 1), pre[c](8, 9), hc[3] if late else mine(3, smr[c]), clip, A.add, A.max)
+        pick("x4", W4 + 16 * me - (24 if me == 0 else 0), 32, "xq", 0, XQW, lst(), ["pt", "pw", "px"])
+    else:
+        serve(3, ["a3"], lo, "x4", W4 + 16 * me, mine(3), clip if poor else None)
+    send("cols3")
+    posk, nk = refills(3, ["a3"])
+    places(3, posk)
+    book(3, nk)
+    d0, n2, d1, g1, g2, lfin = take("bl", 1)(), F(), F(), F(3), F(3), O(3)
+    S(d0, cown[1], AF.Copy, scale=-1.0, bias=16.0)
+    S(n2, cown[1], AF.Identity, bias=cown[2])
+    S(d1, cown[2], AF.Copy, scale=-1.0, bias=16.0)
+    ts(g1(), jw(), cown[1], d0, A.is_ge, A.mult)
+    ts(g2(), jw(), n2, d1, A.is_ge, A.mult)
+    for c in range(3):
+        ts(lfin(c, c + 1), jw(c, c + 1), g1(c, c + 1), g2(c, c + 1), A.add, A.add)
+
+    pick("fin", 0, 48, "cc", 0, 80, lfin())
+    S(R("num", 0, 48), by(sidc(), lfin()), AF.Copy)
+    pick("fin", 48, 64, "x4", 0, 192, lw[3](), ["k3"], ["p3"])
+    mm("py", "vq", 0, "fin", 48, True, True)
+    V(v.tensor_copy, R("ys", 0, 64), R("py", 0, 64))
+    for a, b in ((0, 112),) if half else ((0, 48), (48, 112)):
+        store("y", T.oc[:, 4 * a:4 * b], T.fin[:, a:b].bitcast(u8), R("fin", a, b))
+        for k in range(4):
+            store("sy"[k % 2] if b > 48 else "y", T.osc[4 * k:4 * k + 4, a:b], T.fins[32 * k:32 * k + 4, a:b], R("fins", a, b))
+    store("y", T.sid[0:1, :], T.num[0:1, 0:112], R("num", 0, 112))
+    store("s", T.y[:, :], T.ys[:, :], R("ys", 0, 64))
 
     Q = {"v": v, "s": s, "t": te, "g": g, "y": sy}
-    own = {"v": "vs", "s": "ss", "t": "ts", "g": "gs"}
-    done = {"vs": 0, "ss": 0, "ts": 0, "gs": 0}
-    dmas = {}
-    seen = {q: {} for q in Q}
+    counts, token, seen = {}, {}, {q: {} for q in Q}
 
     def need(q, deps):
         top = {}
@@ -83,349 +676,13 @@ def rank_program(g, core, T, topo):
                 Q[q].wait_ge(T.sem[n], c)
                 seen[q][n] = c
 
-    def run(q, deps, call, *a, **k):
-        need(q, deps)
-        n = own[q]
-        call(*a, **k).then_inc(T.sem[n], 1)
-        done[n] += 1
-        return (n, done[n])
-
-    def V(deps, call, *a, **k):
-        return run("v", deps, call, *a, **k)
-
-    def S(deps, call, *a, **k):
-        return run("s", deps, call, *a, **k)
-
-    def dma(q, deps, sem, out, in_):
-        need(q, deps)
-        Q[q].dma_start(out, in_).then_inc(T.sem[sem], 16)
-        dmas[sem] = dmas.get(sem, 0) + 16
-        return (sem, dmas[sem])
-
-    at = {"fl": 0, "il": 0, "ol": 0}
-
-    def take(buf, n):
-        a = at[buf]
-        at[buf] = a + n + (n % 2 if buf == "ol" else 0)
-        return T[buf][:, a:a + n]
-
-    def F(n):
-        return take("fl", n)
-
-    def I(n):
-        return take("il", n)
-
-    def O(n):
-        return take("ol", n)
-
-    tu = dma("s", [], "lu", T.ut[:, 0:8], T.u[:, 0:8])
-    tqx = dma("y", [], "lqx", T.qt[:, 0:4 * USED], T.qx[:, 0:4 * USED])
-    tw0 = dma("s", [], "lw0", T.wt[:, 0:1536], T.w[:, 0:1536])
-    tx = dma("y", [], "lx", T.xt[:, 0:256], T.x[:, :])
-    tw1 = dma("y", [], "lw1", T.wt[:, 1536:2048], T.w[:, 1536:2048])
-    tv = dma("y", [], "lv", T.vt[:, :], T.v[:, :])
-    tw = [tw0, tw0, tw0, tw1]
-
-    def iota(out, pattern, base, cm, fl):
-        if fl:
-            return run("g", [], g.iota, out, pattern, base, cm, allow_small_or_imprecise_dtypes=True)
-        return run("g", [], g.iota, out, pattern, base, cm)
-
-    a0 = at["fl"]
-    neg, rs0, jw0 = F(7), F(64), F(4)
-    ip, ip2, jp = I(1), I(1), I(64)
-    t_ip = iota(ip, [[0, 1]], 0, 1, False)
-    t_ip2 = iota(ip2, [[0, 1]], 4 * me, 1, False)
-    ngs = []
-    if rank < NR - 1:
-        ngs.append(iota(T.fl[:, a0:a0 + 7 - rank], [[1, 7 - rank]], -7, 0, True))
-    if rank > 0:
-        ngs.append(iota(T.fl[:, a0 + 7 - rank:a0 + 7], [[1, rank]], 1 - rank, 0, True))
-    t_jp = iota(jp, [[1, 64]], 0, -1, False)
-    t_rs = iota(rs0, [[0, 4], [1, 16]], 0, 0, True)
-    t_jw0 = iota(jw0, [[16, 4]], 0, 0, True)
-    ca = at["fl"]
-    c16 = F(64)
-    t_c16 = iota(c16, [[0, 64]], 16, 0, True)
-
-    t_qz = V([], v.memset, T.qt[:, 4 * USED:512], 0.0)
-    t_xz = V([], v.memset, T.xt[:, 256:512], 0.0)
-    t_uz = V([], v.memset, T.ut[:, 12:512], 0.0)
-    O(16)
-    V([], v.memset, T.ol[:, 0:8], 0)
-    t_lo = V([], v.memset, T.ol[:, 8:16], 2)
-    nil = T.sat0[:, 0:1]
-    t_nil = V([], v.memset, nil, 0.0)
-    t_un = S([tu], s.activation, T.ut[:, 8:12], T.ut[:, 4:8], AF.Copy, scale=-1.0)
-    t_a0 = S([t_xz], s.activation, T.at0[:, 256:512], T.xt[:, 256:512], AF.Copy)
-    rst, jd, kh, jq16, hd = F(64), F(4), F(1), F(3), F(1)
-    c_rs = S([t_rs], s.activation, rst, rs0, AF.Sign)
-    t_hd = S([t_nil], s.activation, hd, nil, AF.Copy)
-
-    ik, kcol, ic, dcol = I(1), F(1), I(1), F(1)
-    m7a = at["fl"]
-    mask7, sm = F(7), F(1)
-    ih, isl, hc0a, hc0 = I(1), I(1), F(1), F(1)
-    i16, m16 = I(64), F(64)
-    jwa = at["fl"]
-    jw = F(4)
-    jq = T.fl[:, jwa:jwa + 3]
-    c_ik = V([t_ip], v.tensor_scalar, ik, ip, 15, None, A.bitwise_and)
-    c_ic = V([t_ip2], v.tensor_scalar, ic, ip2, 2, 3, A.logical_shift_right, A.bitwise_and)
-    c_ih = V([t_ip], v.tensor_scalar, ih, ip, 1, 1, A.logical_shift_right, A.bitwise_and)
-    c_k = V([c_ik], v.tensor_copy, kcol, ik)
-    c_is = V([t_ip], v.tensor_scalar, isl, ip, 1, None, A.bitwise_and)
-    c_i16 = V([t_jp], v.tensor_scalar, i16, jp, 15, None, A.bitwise_and)
-
-    wb = 128 * half
-    t_wq = V([tqx, t_qz], v.quantize_mx, T.wq[:, wb:wb + 128], T.wqs[:, wb:wb + 128], T.qt[:, :])
-    need("g", [t_wq])
-    rid, pid = topo.addr(twin, core)
-    g.remote_dma(T.wq[:, wb:wb + USED].bitcast(u8), T.wq[:, wb:wb + USED].bitcast(u8), T.sem.pre, T.sem.loc, pid, rid, topo.mask(core, twin))
-    g.remote_dma(T.wqs[:, wb:wb + USED], T.wqs[:, wb:wb + USED], T.sem.pre, T.sem.loc, pid, rid, topo.mask(core, twin))
-    npre = 2 * len(topo.engines(core, twin))
-    sent = [npre]
-    t_num = [iota(T.num0[:, 0:64], [[1, 64]], PL * rank, 0, True)]
-    t_fill = iota(T.sidc[:, :], [[0, 96]], -1, 0, True)
-
-    t_uq = V([tu, t_uz, t_un], v.quantize_mx, T.uq[:, :], T.uqs[:, :], T.ut[:, :])
-    c_d = V([c_ic], v.tensor_scalar, dcol, ic, float(r0), None, A.add)
-    t_ub = [V([t_uq, t_lo], v.tensor_copy, T.ub[:, :].bitcast(u32), T.uq[:, :].bitcast(u32).indirect(T.ol[:, 8:16])),
-            S([t_uq, t_lo], s.activation, T.ubs[:, :], T.uqs[:, :].indirect(T.ol[:, 8:16]), AF.Copy)]
-    t_ua = [V([], v.tensor_copy, T.ua[:, :].bitcast(u32), T.uq[:, :].bitcast(u32).indirect(T.ol[:, 0:8])),
-            S([], s.activation, T.uas[:, :], T.uqs[:, :].indirect(T.ol[:, 0:8]), AF.Copy)]
-    c_m16 = V([c_i16], v.tensor_scalar, m16, i16, 0.0, None, A.is_equal)
-    c_jw = V([t_jw0, c_k], v.tensor_scalar, jw, jw0, kcol, None, A.add)
-    c_ha = V([c_ih], v.tensor_scalar, hc0a, ih, 128.0 - 0.5, (3.5 - me) / 8.0, A.mult, A.add)
-    c_kh = S([c_k], s.activation, kh, kcol, AF.Copy, bias=0.5)
-    c_jd = S([c_jw], s.activation, jd, jw, AF.Copy, bias=float(BASE), scale=-1.0)
-    c_j16 = S([], s.activation, jq16, jq, AF.Copy, bias=16.0)
-
-    def quant(i):
-        return V([tw[i]], v.quantize_mx, T.wc[:, 128 * i:128 * i + 128], T.wcs[:, 128 * i:128 * i + 128], T.wt[:, 512 * i:512 * i + 512])
-
-    def zeros(n):
-        return V([t_xz], v.quantize_mx, T[n][:, :], T[n + "s"][:, :], T.xt[:, :])
-
-    t_w = [quant(0)]
-    t_X = [V([tx, t_xz], v.quantize_mx, T.x0[:, :], T.x0s[:, :], T.xt[:, :])]
-    t_w += [quant(i) for i in range(1, 4)]
-
-    hc = hc0
-    counts, t_cf, t_lcs, t_lis = [], [], [], []
-    late, ends, books = {}, [], []
-    for t in range(RD):
-        Xc, Xs = T["x%d" % t], T["x%ds" % t]
-        Zc, Zs = T["z%d" % t], T["z%ds" % t]
-        Nc, Ns = T["x%d" % (t + 1)], T["x%ds" % (t + 1)]
-        At, sat, land = T["at%d" % t], T["sat%d" % t], T["cnt%d" % t]
-        num, numn = T["num%d" % t], T["num%d" % (t + 1)]
-        t_mm = [run("t", t_X + [t_w[i]], te.matmul_mx, T["pz%d" % i][:, 0:128], T.wc[:, 128 * i:128 * i + 128],
-                    T.wcs[:, 128 * i:128 * i + 128], Xc[:, 0:128], Xs[:, 0:128], True, True) for i in range(4)]
-        t_r = []
-        for i in range(4):
-            o, z = At[:, i:256:4], T["pz%d" % i][:, 0:64]
-            if i % 2:
-                t_r.append(V([t_mm[i]], v.tensor_scalar, o, z, 0.0, 0.0625, A.max, A.mult))
-            else:
-                t_r.append(S([t_mm[i]], s.activation, o, z, AF.Relu, scale=0.0625))
-        t_z = V(t_r + [t_a0], v.quantize_mx, Zc[:, 0:128], Zs[:, 0:128], At[:, :])
-        if t == 0:
-            c_m7 = V(ngs + [c_d], v.tensor_scalar, mask7, neg, dcol, 0.0, A.add, A.is_gt)
-            c_sm = V([c_d], v.tensor_scalar, sm, dcol, float(rank), 0.125, A.is_gt, A.mult)
-            t_hc = V([c_ha, c_is], v.tensor_tensor, hc0, hc0a, isl, A.add)
-            for k in range(RD):
-                t_nf = S([t_c16], s.activation, T["num%d" % k][:, 64:72], T.fl[:, ca:ca + 8], AF.Copy, scale=-0.0625)
-            for k in range(1, RD):
-                S([t_nil], s.activation, T["sat%d" % k][:, 0:1], nil, AF.Copy)
-            for k in range(1, RD):
-                t_a0 = S([t_xz], s.activation, T["at%d" % k][:, 256:512], T.xt[:, 256:512], AF.Copy)
-        run("t", [t_z] + t_ua, te.matmul_mx, T.ha[:, 0:128], T.ua[:, :], T.uas[:, :], Zc[:, 0:128], Zs[:, 0:128], True, False)
-        t_h = run("t", t_ub, te.matmul_mx, T.ha[:, 0:128], T.ub[:, :], T.ubs[:, :], Zc[:, 0:128], Zs[:, 0:128], False, True)
-        want, cf = F(64), F(1)
-        t_wn = V([t_h], v.tensor_scalar, want, T.ha[:, 0:64], 0.0, None, A.is_gt)
-        t_sat = V([t_wn, t_c16], v.tensor_tensor_scan, sat[:, 1:65], want, c16, 0.0, A.add, A.min)
-        cown = sat[:, 64:65]
-        need("g", [t_sat])
-        slots = {d: 7 - rank if rank > T.rank_of(d) else 6 - rank for d in side + [mate] + other}
-
-        def give(ds, es):
-            ds = [d for d in ds if wanted(rank, d, t)]
-            if not ds:
-                return []
-            sent.append(len(es))
-            sem = T.sem[("ac%d" if early(rank, ds[0]) else "ah%d") % t]
-            return [RemoteDMATransfer(dst_ids=[did(d) for d in ds], dma_engine_mask=bits(es), remote_sem=sem, srcs=[cown],
-                                      dsts=[land[:, slots[d]:slots[d] + 1] for d in ds])]
-
-        ahead = urgent(rank, other[0])
-        now = give(side + other if ahead else side, eoff) + give([mate], eon)
-        tail = [] if ahead else give(other, eoff)
-        if now:
-            g.remote_dma_fused(now, local_sem=T.sem.loc)
-        inc = {d: len(eon) if d == mate else len(eoff) for d in side + [mate] + other if wanted(T.rank_of(d), core, t)}
-        soon = [d for d in inc if early(T.rank_of(d), core)]
-        na, nac = len(soon), sum(inc[d] for d in soon)
-        nah = sum(inc.values()) - nac
-        hcx, stop, satm, encm, sgn, red = F(1), F(64), F(64), F(64), F(64), F(1)
-        sa = at["fl"]
-        seg, encw = F(64), T.fl[:, sa + 15:sa + 64:16]
-        stopw, nine, wid, wj, tww, hdk, bcol = F(4), F(4), F(4), F(4), F(4), F(1), F(1)
-        logo = O(1)
-        t_rd = S([t_sat, c_kh], s.activation, sgn, sat[:, 1:65], AF.Sign, bias=kh, scale=-1.0, accum_out=red)
-        t_cf.append(S([t_sat], s.activation, cf, cown, AF.Copy))
-        counts.append(cf)
-        if t:
-            tot, hdn, hcn = F(1), F(1), F(1)
-            t_to = V(late[t - 1], v.tensor_reduce, tot, T["cnt%d" % (t - 1)][:, 0:7], AxisListType.X, A.add)
-        t_st = V([t_sat], v.tensor_tensor, stop, sat[:, 1:65], sat[:, 0:64], A.subtract)
-        if t:
-            t_hd = V([t_to, t_hd, t_cf[t - 1]], v.tensor_scalar, hdn, tot, counts[t - 1], hd, A.add, A.add)
-        t_sm = V([c_m16], v.tensor_tensor, satm, sat[:, 1:65], m16, A.mult)
-        if t:
-            t_hc = V([t_hd], v.tensor_scalar, hcn, hdn, 0.125, hc0, A.mult, A.add)
-            hd, hc = hdn, hcn
-        t_hk = V([t_hd], v.tensor_scalar, hdk, hd, float(NR - 1), None, A.add)
-        t_em = V([t_sm, t_st], v.tensor_tensor, encm, satm, stop, A.mult)
-        t_hx = V([t_sat, c_sm, t_hc], v.tensor_scalar, hcx, cown, sm, hc, A.mult, A.add)
-        for f in books[:2]:
-            f()
-        t_sg = V([t_em, c_rs], v.tensor_tensor_scan, seg, rst, encm, 0.0, A.mult, A.add)
-        for f in books[2:4]:
-            f()
-        t_sw = V([t_sg], v.tensor_scalar, stopw, encw, 1.0, None, A.min)
-        t_ni = V([t_sg], v.tensor_scalar, nine, encw, 9.0, None, A.is_ge)
-        if t == 0:
-            t_xp = [zeros("x1")]
-            t_cz = zeros("cc")
-            t_xp.append(zeros("x2"))
-        pa = at["fl"]
-        pre, pcol, lst = F(na), T.fl[:, pa + na - 1:pa + na], O(1)
-        mask = T.fl[:, m7a + 7 - na:m7a + 7]
-        P = BASE + QW * me
-        ac = ("ac%d" % t, nac)
-        late[t] = [ac] + ([("ah%d" % t, nah)] if nah else [])
-        t_p = V([ac, c_m7], v.tensor_tensor_scan, pre, land[:, 7 - na:7], mask, 0.0, A.add, A.mult)
-        t_ls = V([t_p, t_hx], v.tensor_scalar, lst, pcol, 0.125, hcx, A.mult, A.add)
-        t_pc = V([t_ls, t_wq, ("pre", npre)], v.tensor_copy, Zc[:, P:P + 16].bitcast(u32), T.wq[:, :].bitcast(u32).indirect(lst))
-        t_ps = S([t_ls, t_wq, ("pre", npre)], s.activation, Zs[:, P:P + 16], T.wqs[:, :].indirect(lst), AF.Copy)
-
-        def codes(via):
-            return [RemoteDMATransfer(dst_ids=[did(peers[e])], dma_engine_mask=bits(via[peers[e]]), remote_sem=T.sem["ak%d" % t],
-                                      srcs=[Zc[:, P + 4 * e:P + 4 * e + 4].bitcast(u8)], dsts=[Zc[:, P:P + 4].bitcast(u8)])
-                    for e in range(1, 4)]
-
-        def scales(via, w):
-            out = []
-            for e in range(1, 4):
-                o = 4 * e if w == 4 else 0
-                out.append(RemoteDMATransfer(dst_ids=[did(peers[e])], dma_engine_mask=bits(via[peers[e]]), remote_sem=T.sem["ap%d" % t],
-                                             srcs=[Zs[:, P + o:P + o + w]], dsts=[Zs[:, P + o - 4 * e:P + o - 4 * e + w]]))
-            return out
-
-        h = len(eon) // 2
-        if t < RD - 1:
-            need("g", [t_pc, t_ps])
-            g.remote_dma_fused(codes({side[0]: eoff[:h], side[1]: eoff[h:2 * h], mate: eon[:h]}) +
-                               scales({side[0]: eoff[2 * h:3 * h], side[1]: eoff[3 * h:], mate: eon[h:]}, 16), local_sem=T.sem.loc)
-            ncol = 3 * h
-        else:
-            via = {side[0]: eoff[:2 * h], side[1]: eoff[2 * h:], mate: eon}
-            need("g", [t_pc])
-            g.remote_dma_fused(codes(via), local_sem=T.sem.loc)
-            need("g", [t_ps])
-            g.remote_dma_fused(scales(via, 4), local_sem=T.sem.loc)
-            ncol = 6 * h
-        sent.append(2 * ncol)
-        if tail:
-            g.remote_dma_fused(tail, local_sem=T.sem.loc)
-        ends += [("ak%d" % t, ncol), ("ap%d" % t, ncol)] + late[t]
-        vi, va, vx, vo = I(4), I(4), F(4), F(4)
-        q = (F(64), F(64), F(64))
-        pl = O(4)
-        t_b = t_hk
-        if rank:
-            pr = F(1)
-            t_pr = V([], v.tensor_reduce, pr, land[:, 7 - rank:7], AxisListType.X, A.add)
-        t_wj = V([t_ni, c_jw], v.tensor_tensor, wj, nine, jw, A.add)
-        t_lg = V([t_rd], v.tensor_scalar, logo, red, 0.5, 32.0, A.mult, A.add)
-        if rank:
-            t_b = V([t_hk, t_pr], v.tensor_tensor, bcol, hdk, pr, A.add)
-        else:
-            bcol = hdk
-        t_wi = V([t_sw, c_jd], v.tensor_tensor, wid, stopw, jd, A.mult)
-        t_vi = V([t_b, t_sg], v.tensor_scalar, vi, encw, bcol, float(2 ** SH + 1), A.add, A.mult)
-        t_tw = V([t_wi, t_wj], v.tensor_tensor, tww, wid, wj, A.add)
-        t_va = V([t_vi], v.tensor_scalar, va, vi, 1, 3 * QW + 2, A.logical_shift_right, A.bitwise_and)
-        for f in books[4:5]:
-            f()
-        t_vx = V([t_va, t_sw], v.tensor_tensor, vx, va, stopw, A.mult)
-        t_vo = V([t_vx, t_tw], v.tensor_tensor, vo, vx, tww, A.add)
-        for f in books[5:]:
-            f()
-        t_pl = V([t_vo], v.tensor_copy, pl, vo)
-        if t == 0:
-            t_xp.append(zeros("x3"))
-            t_vq = V([tv], v.quantize_mx, T.vq[:, :], T.vqs[:, :], T.vt[:, :])
-        ra = 16 + 16 * t
-        t_lks = S([t_lg, t_z, t_cz], s.activation, T.ccs[:, ra:ra + 16], Zs[:, 0:128].indirect(logo), AF.Copy)
-
-        def book(bcol=bcol, t_b=t_b, q=q, t_lg=t_lg, t_z=t_z, t_st=t_st, stop=stop, sat=sat, num=num, numn=numn, ra=ra, logo=logo, Zc=Zc):
-            k = {}
-
-            def b0():
-                t_lcs.append(V([t_lg, t_z, t_cz], v.tensor_copy, T.cc[:, ra:ra + 16].bitcast(u32), Zc[:, 0:128].bitcast(u32).indirect(logo)))
-
-            def b1():
-                k[1] = V([t_b], v.tensor_scalar, q[0], sat[:, 1:65], bcol, float(NR * PL - NR), A.add, A.add)
-
-            def b2():
-                t_lis.append(V(t_num + [t_fill, t_nf], v.tensor_copy, T.sidc[:, ra:ra + 16], num[:, 0:72].indirect(logo)))
-
-            def b3():
-                k[2] = V([k[1]] + t_num, v.tensor_tensor, q[1], q[0], num[:, 0:64], A.subtract)
-
-            def b4():
-                k[3] = V([k[2], t_st], v.tensor_tensor, q[2], q[1], stop, A.mult)
-
-            def b5():
-                t_num[:] = [V([k[3]], v.tensor_tensor, numn[:, 0:64], q[2], num[:, 0:64], A.add)]
-
-            return [b0, b1, b2, b3, b4, b5]
-
-        books = book()
-        if t == RD - 2:
-            d0, n2, d1, g1, g2, l1, l2 = F(1), F(1), F(1), F(3), F(3), F(3), F(3)
-            lfin = O(3)
-            e0 = V([t_cf[1]], v.tensor_scalar, d0, counts[0], -1.0, 16.0, A.mult, A.add)
-            e1 = V([], v.tensor_tensor, n2, counts[0], counts[1], A.add)
-            e2 = V([], v.tensor_scalar, d1, counts[1], -1.0, 16.0, A.mult, A.add)
-            e4 = V([e0, c_jw], v.tensor_scalar, g1, jq, counts[0], d0, A.is_ge, A.mult)
-            e5 = V([e1, e2], v.tensor_scalar, g2, jq, n2, d1, A.is_ge, A.mult)
-            e6 = V([e4, c_j16], v.tensor_tensor, l1, g1, jq16, A.add)
-            e7 = V([e5, e6], v.tensor_tensor, l2, l1, g2, A.add)
-            t_lf = V([e7], v.tensor_copy, lfin, l2)
-        if t == RD - 1:
-            books[0]()
-            t_l2 = S([t_lks, t_lf], s.activation, T.lgs[:, :], T.ccs[:, :].indirect(lfin), AF.Copy)
-            t_l1 = V(t_lcs + [t_lf], v.tensor_copy, T.lg[:, :].bitcast(u32), T.cc[:, :].bitcast(u32).indirect(lfin))
-            dma("y", [t_l1], "st", T.oc[:, 0:192], T.lg[:, :].bitcast(u8))
-            for k in range(4):
-                dma("y", [t_l2], "st", T.osc[4 * k:4 * k + 4, 0:48], T.lgs[32 * k:32 * k + 4, :])
-        t_xc = V([t_pl, ("ak%d" % t, ncol), t_z, t_pc, t_xp[t]], v.tensor_copy, Nc[:, 0:64].bitcast(u32), Zc[:, :].bitcast(u32).indirect(pl))
-        t_xs = S([t_pl, ("ap%d" % t, ncol), t_z, t_ps, t_xp[t]], s.activation, Ns[:, 0:64], Zs[:, :].indirect(pl), AF.Copy)
-        t_X = [t_xc, t_xs]
-    t_y = run("t", t_X + [t_vq], te.matmul_mx, T.py[:, 0:128], T.vq[:, :], T.vqs[:, :], T.x3[:, :], T.x3s[:, :], True, True)
-    dma("y", [t_xc], "st", T.oc[:, 192:448], T.x3[:, 0:64].bitcast(u8))
-    for k in range(4):
-        dma("sy"[k % 2], [t_xs], "st", T.osc[4 * k:4 * k + 4, 48:112], T.x3s[32 * k:32 * k + 4, 0:64])
-    t_yc = S([t_y], s.activation, T.ys[:, :], T.py[:, 0:64], AF.Copy)
-    for f in books[1:4]:
-        f()
-    t_l3 = V(t_lis, v.tensor_copy, T.sidl[:, :], T.sidc[:, :].indirect(lfin))
-    for f in books[4:]:
-        f()
-    dma("y", [t_l3], "st", T.sid[0:1, 0:48], T.sidl[0:1, :])
-    dma("s", [t_yc], "st", T.y[:, :], T.ys[:, :])
-    dma("y", t_num, "st", T.sid[0:1, 48:112], T["num%d" % RD][0:1, 0:64])
-    need("g", list(done.items()) + list(dmas.items()) + [("loc", sum(sent)), ("pre", npre)] + ends)
+    for i in arrange(N):
+        n = N[i]
+        need(n["q"], [token[d] for d in n["deps"] if d in token and not n["q"] == N[d]["q"] == "t"] + [(e, comes[e]) for e in n["ext"]])
+        done = n["fn"]()
+        if n["kind"] != "r":
+            sem, step = (n["sem"], 16) if n["kind"] == "d" else (n["q"] + "s", 1)
+            done.then_inc(T.sem[sem], step)
+            counts[sem] = counts.get(sem, 0) + step
+            token[i] = (sem, counts[sem])
+    need("g", list(counts.items()) + [("loc", sent[0])] + list(comes.items()))

@@ -2,37 +2,38 @@ from concourse.bass import DstId, RemoteDMATransfer
 from concourse.mybir import dt, AluOpType, AxisListType, ActivationFunctionType
 
 NR, PL, CS, RD = 8, 64, 16, 3
-OWN, TWIN, EXTRA, XQW = 448, 192, 576, 592
-SHARE, CUT, POOR, RICH = (40, 48), (24, 32), (3, 2), (0, 3)
+OWN, TWIN, EXTRA, XQW = 384, 896, 960, 976
+SHARE, CUT, POOR, RICH = (40, 48), (24, 39), (3, 2), (0, 3)
 WCODES = (2, 6, 6, 8)
 NCODES = (8, 8, 12)
 W4 = 112
 CODES = "float8_e4m3fn_x4"
-COMES = {"pt": 6.9, "pw": 6.9, "a1": 8.2, "b1": 8.5, "k1": 10.3, "a2": 10.5, "b2": 10.7, "px": 12.0, "k2": 13.1, "c2": 13.6,
-         "late": 16.0, "a3": 16.5, "k3": 18.5, "p3": 18.8}
-LEAVES = {"ahead": 2.2, "count1": 6.8, "cols1": 8.9, "sum1": 9.6, "count2": (9.2, 12.3), "extra": 11.0, "cols2": 11.2,
-          "late2": 14.1, "count3": 14.5, "sum2": 14.8, "cols3": 16.9, "end": 20.2}
-WAKE, ISSUE, LEAST = 0.15, 0.35, 0.09
+COMES = {"pt": (9.0, 7.2), "pw": 6.0, "a1": (8.2, 8.3), "b1": (8.9, 8.2), "k1": (0, 0, 0, 0, 11.0, 11.0, 10.7, 11.0),
+         "a2": (9.6, 10.0, 10.0, 10.0, 10.7, 10.7, 10.9, 10.7), "px": 14.5, "k2": 13.1, "c2": 13.9, "late": 15.9,
+         "a3": 16.25, "k3": 17.6, "p3": 19.4}
+LEAVES = {"ahead": 2.2, "share": (4.0, 7.3), "count1": 6.8, "cols1": 8.9, "count2": (9.2, 12.3), "extra": 13.0, "cols2": (10.6, 10.8),
+          "late2": 13.8, "count3": 14.5, "sum2": 14.9, "cols3": (17.4, 17.5), "end": 19.95}
+WAKE, ISSUE, LEAST = 0.13, 0.35, 0.1
 
 SCRATCH = {
     "wt": ("sbuf", [128, 2048], "bfloat16"), "xt": ("sbuf", [128, 1024], "bfloat16"),
     "ut": ("sbuf", [128, 512], "bfloat16"), "vt": ("sbuf", [128, 512], "bfloat16"),
     "fl": ("sbuf", [128, 3600], "float32"), "il": ("sbuf", [128, 256], "int32"), "ol": ("sbuf", [128, 128], "uint16"),
-    "bl": ("sbuf", [128, 1280], "bfloat16"), "ys": ("sbuf", [128, 64], "float32"), "num": ("sbuf", [128, 128], "float32"),
+    "bl": ("sbuf", [128, 1536], "bfloat16"), "ys": ("sbuf", [128, 64], "float32"), "num": ("sbuf", [128, 208], "float32"),
+    "cnt": ("sbuf", [128, 48], "bfloat16"),
     "ha": ("psum", [128, 512], "float32"), "py": ("psum", [128, 512], "float32"),
 }
 for _n, _w in (("wc", 512), ("uq", 128), ("ua", 128), ("ub", 128), ("vq", 128), ("xq", XQW), ("cc", 128), ("fin", 176),
-               ("x1", 128), ("x2", 192), ("x3", 160), ("x4", 192), ("z2", 128), ("z3", 128)):
+               ("x1", 128), ("x2", 192), ("x3", 176), ("x4", 208), ("x5", 128), ("z2", 128), ("z3", 128)):
     SCRATCH[_n] = ("sbuf", [128, _w], CODES)
     SCRATCH[_n + "s"] = ("sbuf", [128, _w], "uint8")
 for _t in range(1, RD + 1):
     SCRATCH["at%d" % _t] = ("sbuf", [128, 512], "bfloat16")
-    SCRATCH["cnt%d" % _t] = ("sbuf", [128, 16], "bfloat16")
     SCRATCH["out%d" % _t] = ("sbuf", [128, 144], "bfloat16")
 for _t in range(4):
     SCRATCH["pz%d" % _t] = ("psum", [128, 512], "float32")
 SEMAPHORES = ["vs", "ss", "ts", "gs", "lqx", "lu", "lx", "lv", "lw0", "lw1", "st", "loc",
-              "pw", "pt", "px", "a1", "a2", "a3", "b1", "b2", "c2", "k1", "k2", "k3", "p3"]
+              "pw", "pt", "px", "a1", "a2", "a3", "b1", "c2", "k1", "k2", "k3", "p3"]
 
 
 def plan(r, cores, topo):
@@ -50,7 +51,7 @@ def plan(r, cores, topo):
     eoff = topo.engines(core, cores[twin])
     eon = [e for e in topo.engines(core, cores[mate]) if e not in eoff][::2]
 
-    def call(writes):
+    def call(writes, eon=eon):
         out = []
         for es, ws in ((eoff, [w for w in writes if w[0] != mate]), (eon, [w for w in writes if w[0] == mate])):
             groups = []
@@ -84,39 +85,43 @@ def plan(r, cores, topo):
     P = {}
     ws = []
     for a in reversed(first):
-        if a not in (r, twin):
-            ws += both("xq", a, "pw", OWN, 64 * ((r - a - 1) % NR), WCODES[first.index(a)], 8)
+        if a != r:
+            ws += both("xq", a, "pw", OWN, 128 * ((r - a - 5) % NR), WCODES[first.index(a)], 8)
+    P["ahead"] = calls(ws, True)
+    if half:
+        P["ahead"] = P["ahead"][:2] + [call([w for n, w in ws if n == 8 and w[2][0] == k]) for k in ("xqs", "xq")]
     poor = me == POOR[1 - half]
     n = CUT[1 - half] if poor else SHARE[1 - half]
-    tw = both("xq", twin, "pt", OWN, TWIN, n, n)
-    P["ahead"] = calls(tw + ws if half else ws + tw)
-    rich = quad_of(twin)[RICH[1 - half]]
-    P["extra"] = calls(both("xq", rich, "px", OWN + n, EXTRA, 16, 16)) if poor else []
+    nc, ns = (WCODES[me], 8) if half else (0, 0)
+    share = both("xq", twin, "pt", OWN + nc, TWIN + nc, n - nc, 0)[:1] + both("xq", twin, "pt", OWN + ns, TWIN + ns, 0, n - ns)[1:]
+    extra = both("xq", quad_of(twin)[RICH[1 - half]], "px", OWN + n, EXTRA, SHARE[1 - half] - n, SHARE[1 - half] - n) if poor else []
+    P["share"], P["extra"] = (calls(share + extra), []) if half else (calls(share), calls(extra))
 
-    def slot(d, s):
-        others = [j for j in range(NR - 1, -1, -1) if j != d and (d in second or j in first)]
-        return (1 if d in second else 4) + others.index(s)
+    def slot(d, s, t):
+        others = [j for j in range(NR - 1, -1, -1) if j != d]
+        return 16 * t - 16 + (1 if d in second or t == 2 else 0) + others.index(s)
 
     for t in (1, 2, 3):
         if half:
-            ds = [d for d in reversed(quad) if d != r] if t < 3 or me < 3 else []
+            ds = [d for d in reversed(quad) if d != r] + (first if t == 1 else []) if t < 3 or me < 3 else []
         else:
             up, down = [d for d in reversed(quad) if d > r], [d for d in quad if d < r]
+            near = up + down if me < 3 else []
             far = second[3:] + second[:3] if t < 3 else second
-            ds = up + far + down if t == 1 else far + (up + down if t < 3 or me < 3 else [])
-        sem = "c2" if half and t == 2 else "a%d" % t
+            ds = up + far + down if t == 1 else (far[:3] + near + far[3:] if t == 2 else far + near)
+        sem = ("b1", "c2", "a3")[t - 1] if half else "a%d" % t
         src = ("out%d" % t, 63 if t == 1 else 127, 1)
-        ws = [(d, "b%d" % t if d < r and not half and (t == 1 or me == 3) else sem, src, ("cnt%d" % t, slot(d, r), 1)) for d in ds]
+        ws = [(d, "b1" if d < r and not half and t == 1 else sem, src, ("cnt", slot(d, r, t), 1)) for d in ds]
         now = [w for w in ws if w[1] == sem or w[0] == mate]
         P["count%d" % t] = [call(x) for x in (now, [w for w in ws if w not in now]) if x]
-        if half and t < 3:
-            P["sum%d" % t] = [call([(twin, "a%d" % (t + 1), ("out%d" % t, 130, 1), ("cnt%d" % (t + 1), 7, 1))])]
+    if half and me == 3:
+        P["sum2"] = [call([(d, "a3", ("out2", 130 + (d == twin), 1), ("cnt", 39, 1)) for d in first])]
     peers = [quad[(me + e) % 4] for e in range(4)]
 
     def plain(buf, base, sem, sems=None):
         ws = []
         for e in range(1, 4):
-            ws += both(buf, peers[e], sem, base + 16 * me + 4 * e, base + 16 * me, 4, 4, sems)
+            ws += both(buf, peers[e], sem, base + 16 * me + 4 * e, base + 16 * me + (16 if base and peers[e] == second[3] else 0), 4, 4, sems)
         return calls(ws)
 
     P["cols1"] = plain("x2", 0, "k1") if half else []
@@ -126,12 +131,12 @@ def plan(r, cores, topo):
             if j != me:
                 ws += both("x3", quad[j], "k2", 16 * me if me < 3 else 144, 16 * me, NCODES[j], 12)
         P["cols2"] = calls(ws, True)
-        P["late2"] = calls(both("x3", quad[3], "k2", 144 + 4 * (3 - me), 16 * me, 4, 4)) if me < 3 else []
+        P["late2"] = [call([w for n, w in both("x3", quad[3], "k2", 144 + 4 * (3 - me), 16 * me, 4, 16)], eoff)] if me < 3 else []
     else:
         P["cols2"] = plain("x3", 0, "k2")
     if me == RICH[half]:
         order = [1, 2, 3, 0] if me == 0 else [3, 0, 1, 2]
-        base = W4 + 16 * me - 8 * order.index(me)
+        base = W4 + 16 * half + 16 * me - 8 * order.index(me)
         ws = []
         for e, j in enumerate(order):
             if j != me:
@@ -150,7 +155,7 @@ def arrange(N):
     ready = [i for i, n in enumerate(N) if not left[i]]
     while ready:
         est = {i: max([free.get(N[i]["q"], 0.0), N[i]["from"]] +
-                      [N[d]["end"] + (0.0 if N[d]["q"] == N[i]["q"] == "t" or N[d]["kind"] == "r" else WAKE) for d in N[i]["deps"]]) for i in ready}
+                      [N[d]["end"] + (0.0 if d in N[i]["behind"] or N[d]["kind"] == "r" else WAKE) for d in N[i]["deps"]]) for i in ready}
         a = min(ready, key=lambda i: est[i] + N[i]["dur"])
         i = min([j for j in ready if N[j]["q"] == N[a]["q"] and est[j] < est[a] + N[a]["dur"]], key=lambda j: (N[j]["last"], j))
         free[N[i]["q"]] = est[i] + N[i]["dur"]
@@ -187,6 +192,9 @@ def rank_program(g, core, T, topo):
 
     N, seen_by, sent = [], {}, [0]
 
+    def when(x):
+        return x[rank if len(x) == NR else half] if isinstance(x, tuple) else x
+
     def R(name, a, b, st=1):
         ap = T[name][:, a:b:st] if st > 1 else T[name][:, a:b]
         psum = SCRATCH[name][0] == "psum"
@@ -198,7 +206,7 @@ def rank_program(g, core, T, topo):
     def by(w, off):
         return (w[0].indirect(off[0]), w[1], w[2], w[3], 16 * off[4], off)
 
-    def note(q, kind, fn, outs, ins, dur, lat=None, ext=(), after=(), last=99.0, sem=None):
+    def note(q, kind, fn, outs, ins, dur, lat=None, ext=(), after=(), last=99.0, sem=None, behind=()):
         i = len(N)
         deps = set(after)
         ins = ins + [x[5] for x in outs + ins if x[5]]
@@ -207,14 +215,16 @@ def rank_program(g, core, T, topo):
                 if (w or jw) and a < x[3] and x[2] < b and j != i:
                     deps.add(j)
             seen_by[x[1]].append((i, x[2], x[3], w))
+        behind = [d for d in behind if d not in deps] + [d for d in deps if q == N[d]["q"] == "t"]
+        deps |= set(behind)
         ext = [e for e in ext if e in comes]
         N.append({"q": q, "kind": kind, "fn": fn, "deps": sorted(deps), "next": [], "dur": dur, "lat": lat or dur, "ext": ext, "sem": sem,
-                  "from": max([0.0] + [COMES["late" if late and e == "k2" else e] for e in ext]), "last": last})
+                  "from": max([0.0] + [when(COMES["late" if late and e == "k2" else e]) for e in ext]), "last": last, "behind": behind})
         for d in deps:
             N[d]["next"].append(i)
         return i
 
-    def op(q, call, *a, outs=1, ext=(), after=(), dur=None, both=False, **k):
+    def op(q, call, *a, outs=1, ext=(), after=(), dur=None, both=False, last=99.0, behind=(), **k):
         views = [x for x in a if isinstance(x, tuple)]
         o = views[:outs] + [k[x] for x in k if x == "accum_out"]
         i = views[outs:] + [k[x] for x in k if x != "accum_out" and isinstance(k[x], tuple)]
@@ -228,7 +238,7 @@ def rank_program(g, core, T, topo):
                 dur = max(LEAST, 0.001 * max(x[4] for x in views) * (2 if both else 1))
         a2 = [x[0] if isinstance(x, tuple) else x for x in a]
         k2 = {x: k[x][0] if isinstance(k[x], tuple) else k[x] for x in k}
-        return note(q, "c", lambda: call(*a2, **k2), o, i, dur, ext=ext, after=after)
+        return note(q, "c", lambda: call(*a2, **k2), o, i, dur, ext=ext, after=after, last=last, behind=behind)
 
     def V(call, *a, **k):
         return op("v", call, *a, **k)
@@ -239,11 +249,11 @@ def rank_program(g, core, T, topo):
     def ts(out, a, s1, s2, o0, o1=None, **k):
         return V(v.tensor_scalar, out, a, s1, None, o0, **k) if o1 is None else V(v.tensor_scalar, out, a, s1, s2, o0, o1, **k)
 
-    def quant(dst, a, n, src, b):
-        return V(v.quantize_mx, R(dst, a, a + n), R(dst + "s", a, a + n), R(src, b, b + 4 * n), outs=2, dur=0.012 + 0.00088 * n)
+    def quant(dst, a, n, src, b, **k):
+        return V(v.quantize_mx, R(dst, a, a + n), R(dst + "s", a, a + n), R(src, b, b + 4 * n), outs=2, dur=0.012 + 0.00088 * n, **k)
 
-    def mm(out, w, a, x, b, start, stop, **k):
-        return op("t", te.matmul_mx, R(out, 0, 128), R(w, a, a + 128), R(w + "s", a, a + 128), R(x, b, b + 128), R(x + "s", b, b + 128),
+    def mm(out, w, a, x, b, start, stop, n=128, **k):
+        return op("t", te.matmul_mx, R(out, 0, n), R(w, a, a + 128), R(w + "s", a, a + 128), R(x, b, b + n), R(x + "s", b, b + n),
                   start, stop, dur=0.09, **k)
 
     def iota(out, pattern, base, cm=0):
@@ -253,11 +263,10 @@ def rank_program(g, core, T, topo):
     def load(q, sem, dst, src, lat, last, **k):
         return note(q, "d", lambda: (s if q == "s" else sy).dma_start(dst[0], src), [dst], [], 0.05, lat, sem=sem, last=last, **k)
 
-    def store(q, dst, src, reads):
-        return note(q, "d", lambda: (s if q == "s" else sy).dma_start(dst, src), [], [reads], 0.05, sem="st", last=LEAVES["end"])
+    def store(q, dst, src, reads, more=0.0):
+        return note(q, "d", lambda: (s if q == "s" else sy).dma_start(dst, src), [], [reads], 0.2, sem="st", last=LEAVES["end"] + more)
 
     def send(name, after=()):
-        last = LEAVES[name][half] if isinstance(LEAVES[name], tuple) else LEAVES[name]
         for m, c in enumerate(P.get(name, [])):
             def raw(x):
                 a = T[x[0]][:, x[1]:x[1] + x[2]]
@@ -269,7 +278,7 @@ def rank_program(g, core, T, topo):
                                              remote_sem=T.sem[sem], srcs=[raw(src)], dsts=[raw(dst) for d, dst in ds]))
                 sent[0] += len(es)
             note("g", "r", lambda trs=trs: g.remote_dma_fused(trs, local_sem=T.sem.loc), [],
-                 [R(x[2][0], x[2][1], x[2][1] + x[2][2]) for x in c], ISSUE, after=after, last=last + ISSUE * m)
+                 [R(x[2][0], x[2][1], x[2][1] + x[2][2]) for x in c], ISSUE, after=after, last=when(LEAVES[name]) + ISSUE * m)
 
     at = {"fl": 0, "il": 0, "ol": 0, "bl": 0}
 
@@ -288,17 +297,17 @@ def rank_program(g, core, T, topo):
     def O(n=1):
         return take("ol", n)
 
-    def pick(dst, a, n, src, lo, hi, lst, ext=(), exts=None):
-        V(v.tensor_copy, words(dst, a, a + n), by(words(src, lo, hi), lst), ext=ext)
+    def pick(dst, a, n, src, lo, hi, lst, ext=(), exts=None, behind=()):
+        V(v.tensor_copy, words(dst, a, a + n), by(words(src, lo, hi), lst), ext=ext, behind=behind)
         S(R(dst + "s", a, a + n), by(R(src + "s", lo, hi), lst), AF.Copy, ext=exts or ext)
 
     load("s", "lu", R("ut", 0, 8), T.u[:, 0:8], 1.6, -5.0)
     load("y", "lqx", R("xt", 256, 448), T.qx[:, 0:192], 1.9, -5.0)
-    load("s", "lw0", R("wt", 0, 1536), T.w[:, 0:1536], 3.7, -4.0)
-    load("y", "lx", R("xt", 0, 256), T.x[:, :], 3.9, -4.0)
-    load("y", "lw1", R("wt", 1536, 2048), T.w[:, 1536:2048], 4.5, -3.0)
+    load("s", "lw0", R("wt", 0, 1536), T.w[:, 0:1536], 3.0, -4.0)
+    load("y", "lx", R("xt", 0, 256), T.x[:, :], 3.2, -4.0)
+    load("y", "lw1", R("wt", 1536, 2048), T.w[:, 1536:2048], 3.8, -3.0)
 
-    ip, ip2, neg, rs0, row, jw0 = I(), I(), F(3), F(64), F(80), F(3)
+    ip, ip2, neg, rs0, long = I(), I(), F(3), F(64), F(128)
     iota(ip, [[0, 1]], 0, 1)
     iota(ip2, [[0, 1]], 4 * me, 1)
     iota(rs0(), [[0, 4], [1, 16]], 0)
@@ -306,18 +315,31 @@ def rank_program(g, core, T, topo):
         iota(neg(0, 3 - me), [[1, 3 - me]], -3)
     if me > 0:
         iota(neg(3 - me, 3), [[1, me]], 1 - me)
-    iota(row(), [[1, 80]], 0)
-    iota(jw0(), [[16, 3]], 0)
+    iota(long(48 if half else 0, 128), [[1, 80 if half else 128]], 0 if half else -48)
+
+    def row(a=0, b=80):
+        return long(48 + a, 48 + b)
+
     krow = rs0(0, 16)
     V(v.memset, R("xt", 448, 1024), 0.0, dur=0.3)
-    lua, lub, lw = O(8), O(8), {1: O(5), 2: O(5), 3: O(4)}
+    lua, lw = O(8), {1: O(5), 2: O(5), 3: O(4)}
     V(v.memset, lua(), 0)
-    V(v.memset, lub(), 2)
-    c16, mk, seed, zero = take("bl", 128), F(9), F(16), F(64)
+    caps, mk, seed = take("bl", 192), F(9), F(16)
+
+    def c16(a=0, b=128):
+        return caps(64 + a, 64 + b)
+
     V(v.memset, seed(), 2.0 ** 60)
-    fills = [quant("x2", 0, 128, "xt", 448), quant("x4", 0, 128, "xt", 448), quant("x3", 0, 144, "xt", 256)]
+    fills, later = [quant("x2", 0, 128, "xt", 448)], []
+    (fills if half or me == 3 else later).append(quant("x3", 0, 176, "xt", 256))
+    later.append(quant("x4", 0, 128, "xt", 448))
     quant("cc", 0, 128, "xt", 448)
-    quant("fin", 48, 128, "xt", 256)
+    if late:
+        later.append(quant("x4", 80, 128, "xt", 256))
+        quant("x5", 0, 128, "xt", 256)
+        S(R("at3", 256, 512), R("xt", 448, 704), AF.Copy)
+    else:
+        quant("fin", 48, 128, "xt", 256)
     ik, kcol, kcol2, ic, dcol, ih, isl, b3, hc0a, hc0, sm, m16 = I(), F(), F(), I(), F(), I(), I(), I(), F(), F(), F(), F(64)
     ts(ik, ip, 15, None, A.bitwise_and)
     ts(ic, ip2, 2, 3, A.logical_shift_right, A.bitwise_and)
@@ -337,47 +359,55 @@ def rank_program(g, core, T, topo):
     ts(hc0, isl, hc0a, None, A.add)
     ts(m16(), rs0(), kcol, None, A.is_equal)
     for t in (1, 2):
-        V(v.memset, lw[t](4, 5), 128)
-    want = {t: take("bl", 144) for t in (1, 2, 3)}
-    S(R("ut", 12, 512), R("xt", 448, 948), AF.Copy)
+        V(v.memset, lw[t](4, 5), 448 - 128 * t)
+    wants = take("bl", 336)
+    want = {t: (lambda a, b, o=o: wants(o + a, o + b)) for t, o in ((1, 256), (2, 0), (3, 256 if late else 128))}
+    S(R("ut", 8, 512), R("xt", 448, 952), AF.Copy)
     S(R("at1", 256, 512), R("xt", 448, 704), AF.Copy)
     big, rst, kh, hbig, nbig, k512, jw = F(16), F(64), F(), F(), F(), F(16), F(3)
     S(big(), seed(), AF.Square)
+    bigb = take("bl", 1)()
+    S(bigb, big(0, 1), AF.Copy)
     S(rst(), rs0(), AF.Sign)
     S(kh, kcol, AF.Copy, bias=0.5)
-    S(hbig, big(0, 1), AF.Copy, scale=0.5)
-    S(nbig, big(0, 1), AF.Copy, scale=-0.5)
+    if half and not late:
+        S(hbig, big(0, 1), AF.Copy, scale=0.5)
+        S(nbig, big(0, 1), AF.Copy, scale=-0.5)
     S(k512(), krow, AF.Copy, bias=float(NR * PL))
-    S(jw(), jw0(), AF.Identity, bias=kcol)
+    S(jw(), long(48, 96, 16), AF.Identity, bias=kcol)
 
     def num(a=0, b=80):
         return R("num", 48 + a, 48 + b)
 
-    sidc, lrow, thr = F(80), {t: F(80) for t in (1, 2, 3)}, {2: F(144), 3: F(144)}
+    sidc, lrow, thr = (lambda a=0, b=80: R("num", 128 + a, 128 + b)), {1: F(80), 2: F(80), 3: row}, {2: F(144), 3: F(144)}
     S(num(0, 64), row(0, 64), AF.Copy, bias=float(PL * rank))
-    S(num(64, 80), row(0, 16), AF.Copy, bias=-1.0, scale=0.0)
-    S(sidc(48, 80), row(0, 32), AF.Copy, bias=-1.0, scale=0.0)
-    S(zero(), row(0, 64), AF.Copy, scale=0.0)
+    S(R("num", 112, 208), R("xt", 448, 544), AF.Copy, bias=-1.0)
     wide = {2: not half, 3: half and not late}
     for t in (2, 3):
-        if wide[t]:
-            S(thr[t](64, 144), row(), AF.Copy, scale=0.0)
-        elif not (late and t == 3):
-            for a in (0, 64):
-                S(thr[t](a, a + 64), row(0, 64), AF.Identity, scale=0.0, bias=big(0, 1))
-    for t in (1, 2, 3):
-        S(R("cnt%d" % t, 8, 9), row(0, 1), AF.Copy)
-        S(want[t](64, 80) if t == 1 else want[t](128, 144), row(0, 16), AF.Copy, bias=1.0, scale=0.0)
-        S(lrow[t](), row(), AF.Copy, bias=64.0 if t < 3 else 0.0)
+        if not (late and t == 3):
+            S(thr[t](64, 144), R("xt", 448, 528), AF.Copy)
+            if not wide[t]:
+                S(thr[t](0, 64), R("xt", 448, 512), AF.Identity, bias=big(0, 1))
+    V(v.memset, R("cnt", 8, 48, 16), 0.0)
+    V(v.memset, wants(320, 336), 1.0)
+    for t in (1, 2):
+        S(lrow[t](), row(), AF.Copy, bias=64.0)
     S(c16(), R("xt", 448, 576), AF.Copy, bias=16.0)
     hp = POOR[half] + 4 * (1 - half)
     pt, n8 = F(800), 8 * SHARE[half]
+    iota(pt(0, 64), [[0, 8], [2, 2], [16, 4]], 0)
+    for a, b in ((64, 128), (128, 256), (256, n8)):
+        S(pt(a, b), pt(0, b - a), AF.Copy)
+    V(v.memset, pt(8 * CUT[half] + hp, n8, 8), 16.0 * RICH[half] + 4)
+    S(pt(400, 400 + n8), pt(0, n8), AF.Copy, bias=1.0)
 
     quant("xq", OWN, 128, "xt", 256)
     send("ahead")
-    S(R("ut", 8, 12), R("ut", 4, 8), AF.Copy, scale=-1.0)
+    if not half:
+        send("share")
+    S(R("ut", 128, 132), R("ut", 4, 8), AF.Copy, scale=-1.0)
     quant("uq", 0, 128, "ut", 0)
-    pick("ub", 0, 128, "uq", 0, 128, lub())
+    pick("ub", 0, 128, "uq", 32, 128, lua())
     pick("ua", 0, 128, "uq", 0, 128, lua())
     quant("x1", 0, 128, "xt", 0)
     for i in range(4):
@@ -387,15 +417,15 @@ def rank_program(g, core, T, topo):
     sat[1] = lambda: R("out1", 0, 80)
     cown = {t: R("out%d" % t, 63 if t == 1 else 127, 64 if t == 1 else 128) for t in (1, 2, 3)}
     logo = {t: O() for t in (1, 2, 3)}
-    hd, hc = {}, {1: hc0}
+    hd, hc, signs = {}, {1: hc0}, []
 
     def land(t, a, b):
-        return R("cnt%d" % t, a, b)
+        return R("cnt", 16 * t - 16 + a, 16 * t - 16 + b)
 
     def layer(t, ext=()):
-        n = 64 if t == 1 else 128
+        n = 64 if t == 1 or late and t == 3 else 128
         for i in range(4):
-            mm("pz%d" % i, "wc", 128 * i, "x%d" % t, 0, True, True, ext=ext)
+            mm("pz%d" % i, "wc", 128 * i, "x5" if late and t == 3 else "x%d" % t, 0, True, True, ext=ext)
         for i in range(4):
             o, z = R("at%d" % t, i, 4 * n, 4), R("pz%d" % i, 0, n)
             o = o[:1] + ("at%d.%d" % (t, i),) + o[2:]
@@ -403,38 +433,36 @@ def rank_program(g, core, T, topo):
                 ts(o, z, 0.0, 0.0625, A.max, A.mult)
             else:
                 S(o, z, AF.Relu, scale=0.0625)
-        dst, a = ("x2", 64) if t == 1 else ("z%d" % t, 0)
+        dst, a = ("x2", 64) if t == 1 else ("x4", 0) if late and t == 3 else ("z%d" % t, 0)
         j = len(N)
         V(v.quantize_mx, R(dst, a, a + 128), R(dst + "s", a, a + 128), R("at%d" % t, 0, 512), outs=2, dur=0.125, after=range(j - 4, j))
         mm("ha", "ua", 0, dst, a, True, False)
         mm("ha", "ub", 0, dst, a, False, True)
 
-    def count(t):
-        if t == 1:
-            ts(want[1](0, 64), R("ha", 0, 64), 0.0, None, A.is_gt)
-            V(v.tensor_tensor_scan, sat[1](), want[1](0, 80), c16(0, 80), 0.0, A.add, A.min)
-        elif late and t == 3:
-            ts(want[t](0, 128), R("ha", 0, 128), 0.0, None, A.is_gt)
-        else:
-            V(v.tensor_tensor, want[t](0, 128), R("ha", 0, 128), thr[t](0, 128), A.is_gt)
-            V(v.tensor_tensor_scan, R("out%d" % t, 0, 128), want[t](0, 128), c16(), 0.0, A.add, A.min, dur=LEAST)
+    def count(t, cap=c16):
+        if t == 1 or late and t == 3:
+            ts(want[t](0, 64), R("ha", 0, 64), 0.0, None, A.is_gt)
+            return V(v.tensor_tensor_scan, sat[t](), want[t](0, 80), c16(0, 80), 0.0, A.add, A.min)
+        V(v.tensor_tensor, want[t](0, 128), R("ha", 0, 128), thr[t](0, 128), A.is_gt)
+        return V(v.tensor_tensor_scan, R("out%d" % t, 0, 128), want[t](0, 128), cap(), 0.0, A.add, A.min, dur=LEAST)
 
     def stops(t):
         wg, red = take("bl", 80), F()
-        if t > 1:
-            S(wg(), by(want[t](0, 144), lw[t - 1]()), AF.Copy)
+        if t > 1 and not (late and t == 3):
+            S(wg(), by(want[t](0, 592 - 128 * t), lw[t - 1]()), AF.Copy)
             V(v.tensor_tensor_scan, sat[t](), wg(), c16(0, 80), 0.0, A.add, A.min)
-        S(F(80)(), sat[t](), AF.Sign, bias=kh, scale=-1.0, accum_out=red)
+        signs.append(S(F(80)(), sat[t](), AF.Sign, bias=kh, scale=-1.0, accum_out=red))
         ts(logo[t](), red, 0.5, 40.0, A.mult, A.add)
 
-    def add_up(t, a, b, ext):
+    def add_up(t, a, b, ext, wait=0.0):
         o = F()
-        S(F(8)(0, b - a), land(t, a, b), AF.Identity, accum_out=o, ext=ext)
+        N[S(F(8)(0, b - a), land(t, a, b), AF.Identity, accum_out=o, ext=ext)]["from"] += wait
         return o
 
     def head(t):
         hd[t], hc[t], o = F(), F(), F()
-        tot = add_up(t - 1, c0, 7 if t == 2 and not half else 8, ["a%d" % (t - 1), "b%d" % (t - 1)] + (["c2"] if t == 3 else []))
+        a, b = (1, 8) if half else (0, 7) if t == 2 else (5 if me == 3 else 6, 8)
+        tot = add_up(t - 1, a, b, ["a1", "b1"] if t == 2 else ["a2", "c2"])
         if t == 2:
             S(hd[t], tot, AF.Identity, bias=cown[1])
         else:
@@ -449,25 +477,29 @@ def rank_program(g, core, T, topo):
 
     def serve(t, ext, lo, dst, a, h, clip=None):
         pre, lst = F(9), O()
-        V(v.tensor_tensor_scan, pre(lo, 9), land(t, lo, 9), mk(lo, 9), 0.0, A.add, A.mult, ext=ext)
-        if clip is None:
-            ts(lst(), pre(8, 9), h, None, A.add)
+        if t == 2 and not half:
+            V(v.tensor_tensor_scan, pre(lo, 8), land(t, lo, 8), mk(lo - 1, 7), 0.0, A.add, A.mult, ext=ext)
+            ts(lst(), pre(7, 8), 0.125, h, A.mult, A.add)
         else:
-            ts(lst(), pre(8, 9), h, clip, A.add, A.min)
+            V(v.tensor_tensor_scan, pre(lo, 9), land(t, lo, 9), mk(lo, 9), 0.0, A.add, A.mult, ext=ext)
+            if clip is None:
+                ts(lst(), pre(8, 9), h, None, A.add)
+            else:
+                ts(lst(), pre(8, 9), h, clip, A.add, A.min)
         pick(dst, a, 16, "xq", 0, EXTRA, lst(), ["pt", "pw"])
 
     def refills(t, ext, o=None):
         lp, l2, mrow, posk, nk, st = O(), O(), F(16), F(16), F(16), F()
-        pr = add_up(t, c0 + 3 - me, 8, ext)
+        pr = add_up(t, c0 + 3 - me + (t == 2 and not half), 8, ext) if half or me or t == 3 else None
         k = kcol2 if o is None else kcol
-        if t == 1:
-            ts(lp(), k, pr, None, A.add)
-            st = pr
+        if t == 1 or pr is None:
+            st = pr or hd[t]
+            ts(lp(), k, st, None, A.add, ext=ext)
         else:
             ts(lp(), k, pr, hd[t], A.add, A.add)
             S(st, pr, AF.Identity, bias=hd[t])
         if o is None:
-            S(posk(), by(pt(), lp()), AF.Copy, bias=float(W4 if t == 3 else 0))
+            S(posk(), by(pt(), lp()), AF.Copy, bias=float(W4 + 16 * late if t == 3 else 0))
         else:
             ts(l2(), kcol, o, None, A.add, ext=ext)
             S(mrow(), by(mt(), l2()), AF.Copy)
@@ -482,8 +514,14 @@ def rank_program(g, core, T, topo):
         V(v.tensor_tensor_scan, sg(), rst(), lm(), 0.0, A.mult, A.add)
         V(v.tensor_copy, lw[t](0, 4), sg(15, 64, 16))
 
-    def gate(t):
-        V(v.tensor_copy, by(thr[t](0, 128), lw[t - 1](0, 4)), zero())
+    def gate(t, posk):
+        dg, pw, lg, vk = F(16), F(), O(), F(16)
+        V(v.tensor_copy, by(thr[t](64, 144), logo[t - 1]()), big())
+        V(v.tensor_tensor, dg(), posk(), m16(0, 16), A.mult)
+        S(F(16)(), dg(), AF.Identity, accum_out=pw)
+        V(v.tensor_copy, lg(), pw)
+        ts(vk(), krow, cown[t - 1], bigb, A.is_ge, A.mult)
+        V(v.tensor_copy, by(thr[t](0, 64), lg()), vk())
 
     def order(t):
         pick("x%d" % (t + 1), 64 if t < 3 else 0, 64, "z%d" % t, 0, 128, lw[t - 1](0, 4))
@@ -494,35 +532,24 @@ def rank_program(g, core, T, topo):
         S(sidc(16 * t - 16, 16 * t), by(num(), logo[t]()), AF.Copy)
         V(v.tensor_copy, by(num(), logo[t]()), nk())
         if t < 3:
-            S(num(64, 80), row(0, 16), AF.Copy, bias=-1.0, scale=0.0)
+            S(num(64, 80), R("xt", 448, 464), AF.Copy, bias=-1.0)
 
-    def window(t, kx, shift, sem):
-        hn, hb, kp, dd, o = F(), F(), F(64), F(64), F()
-        V(v.tensor_copy, by(thr[t](64, 144), logo[t - 1]()), big())
-        S(hn, cown[t - 1], AF.Copy, scale=-0.5, bias=0.5 - shift)
-        S(hb, cown[t - 1], AF.Identity, scale=nbig, bias=hbig)
-        S(kp(), kx, AF.Identity, bias=hn)
-        if me == 0:
-            o = 0.0
-        elif me == 1:
-            o = land(t - 1, c0 + 2, c0 + 3)
-        elif me == 2:
-            S(o, land(t - 1, c0 + 1, c0 + 2), AF.Identity, bias=land(t - 1, c0 + 2, c0 + 3), ext=[sem])
-        else:
-            o = add_up(t - 1, c0, c0 + 3, [sem])
-        S(dd(), kp(), AF.Abs, scale=-1.0, bias=o, ext=[sem] if me else [])
-        S(thr[t](0, 64), dd(), AF.Relu, scale=big(0, 1), bias=hb)
+    def below(t, sem):
+        V(v.tensor_copy, by(thr[t + 1](64, 144), logo[t]()), big())
+        if me < 2:
+            return land(t, c0 + 2, c0 + 3) if me else 0.0
+        if me == 3:
+            return add_up(t, c0, c0 + 3, [sem])
+        o = F()
+        S(o, land(t, c0 + 1, c0 + 2), AF.Identity, bias=land(t, c0 + 2, c0 + 3), ext=[sem])
         return o
-
-    def total(t, sem):
-        S(R("out%d" % t, 130, 131), add_up(t, 1, 4, [sem]), AF.Identity, bias=cown[t])
-        send("sum%d" % t)
 
     clip, hcr, mkr, smr = F(), F(), [F(9), F(9)], [F(), F()]
     if poor:
         top = TWIN + CUT[half] - 1.0
         ts(clip, ih, (top - 4095.0) * (-1 if half else 1), top if half else 4095.0, A.mult, A.add)
     if rich:
+        mark = len(N)
         turn = [1, 2, 3, 0] if me == 0 else [3, 0, 1, 2]
         i3, t1, t2, t3 = I(), F(), F(), F()
         v0, v1, v2 = loc[0] + (3.5 - me) / 8.0, loc[1] + (3.5 - me - 4) / 8.0, EXTRA - CUT[half] + (3.5 - hp) / 8.0
@@ -539,43 +566,50 @@ def rank_program(g, core, T, topo):
         ts(clip, i3, 2.0, float(EXTRA), A.is_equal, A.mult)
         ts(t3, isl, t1, t2, A.add, A.add)
         S(hcr, t3, AF.Copy, bias=v0)
+        for n in N[mark:] if not late else []:
+            n["from"] = 13.5
 
     layer(1)
-    count(1)
+    counted = count(1)
     send("count1", fills)
-    iota(pt(0, n8), [[0, n8 // 8], [2, 2], [16, 4]], 0)
-    V(v.memset, pt(8 * CUT[half] + hp, n8, 8), 16.0 * RICH[half] + 4)
-    S(pt(400, 400 + n8), pt(0, n8), AF.Copy, bias=1.0)
+    if half:
+        send("share", [len(N) - 1])
     stops(1)
     if not half:
         ipw, two, wa, wc0, wc1, lwin, posk, nk = I(), F(4), I(), F(), F(), O(4), F(16), F(16)
-        iota(ipw, [[0, 1]], NR - 1 - me, 1)
+        iota(ipw, [[0, 1]], NR - 5 - me, 1)
         iota(two(), [[2, 4]], 0)
         ts(wa, ipw, 7, None, A.bitwise_and)
-        ts(wc0, wa, 64.0, None, A.mult)
+        ts(wc0, wa, 128.0, None, A.mult)
         ts(wc1, b3, wc0, None, A.add)
         ts(lwin(), two(), wc1, None, A.add)
-        w0 = 48 - 16 * me
-        pick("x2", w0, 64 - w0, "xq", 0, EXTRA, lwin(0, me + 1), ["pt", "pw"])
-        o = window(2, row(0, 64), float(w0), "a1")
+        w0, ext = 48 - 16 * me, ["a1"] if me else []
+        pick("x2", w0, 64 - w0, "xq", 0, TWIN + WCODES[me], lwin(0, me + 1), ["pw"], behind=[counted])
+        kq, hq = F(64), F()
+        S(hq, cown[1], AF.Copy, scale=-1.0, bias=0.5 - w0)
+        S(kq(), row(0, 64), AF.Identity, bias=hq)
+        o = below(1, "a1")
+        ts(thr[2](0, 64), kq(), o, bigb if me == 1 else big(0, 1), A.is_gt, A.mult, ext=ext)
+        ts(caps(0, 64), row(-w0, 64 - w0), o, 16.0, A.is_ge, A.mult, ext=ext)
         layer(2)
-        count(2)
-        send("count2")
-        send("extra")
-        kw = F(16)
-        S(kw(), krow, AF.Copy, bias=float(w0))
-        S(posk(), kw(), AF.Identity, bias=o, ext=["a1"] if me else [])
-        S(nk(), k512(), AF.Identity, bias=o, ext=["a1"] if me else [])
+        count(2, lambda: caps(0, 128))
+        send("count2", later)
+        S(posk(), row(w0, w0 + 16), AF.Identity, bias=o, ext=ext)
+        S(nk(), k512(), AF.Identity, bias=o, ext=ext)
         places(1, posk)
         book(1, nk)
         head(2)
         order(2)
         stops(2)
-        serve(2, ["a2"], c0 if me == 3 else c0 + 1, "x3", 16 * me, mine(2))
+        serve(2, ["a2"], c0 + 1 if me == 3 else c0 + 2, "x3", 16 * me, mine(2))
         send("cols2")
+        send("extra", [len(N) - 1])
         posk, nk = refills(2, ["a2"])
         places(2, posk)
-        gate(3)
+        mark = len(N)
+        gate(3, posk)
+        for n in N[mark:]:
+            n["from"] = when(LEAVES["cols2"])
         layer(3, ["k2"])
         count(3)
         send("count3")
@@ -583,36 +617,39 @@ def rank_program(g, core, T, topo):
         e4, hcn, hcn2 = I(), F(), F()
         ts(e4, ip, 2, 3, A.logical_shift_right, A.bitwise_and)
         ts(hcn, e4, 2.0, hc0, A.mult, A.add)
-        serve(1, ["a1"], c0, "x2", 16 * me, mine(1))
+        serve(1, ["a1", "b1"], c0, "x2", 16 * me, mine(1))
         send("cols1")
-        total(1, "a1")
-        send("extra")
-        posk, nk = refills(1, ["a1"])
+        posk, nk = refills(1, ["a1", "b1"])
         places(1, posk)
         book(1, nk)
         head(2)
-        gate(2)
         S(hcn2, hd[2], AF.Identity, scale=0.125, bias=hcn)
         serve(2, ["a2"], 4, "x3", 144 if late else 16 * me, hcn2)
         send("cols2")
+        gate(2, posk)
         layer(2, ["k1"])
         order(2)
         count(2)
-        send("count2")
+        send("count2", later)
         stops(2)
         serve(2, ["a2", "c2"], c0, "x3", 48 if late else 144, mine(2))
         send("late2")
         if not late:
-            hm, m8, mt, ki, kj, kx = F(64), F(64), F(64), I(64), I(64), F(64)
+            hm, m8, mt, ki, kj, kx, hn, hb, kp, dd = F(64), F(64), F(64), I(64), I(64), F(64), F(), F(), F(64), F(64)
             for b in (0, 1):
                 iota(hm(b, 64, 2), [[1, 4], [0, 4], [4, 2]], 512)
                 iota(m8(b, 64, 2), [[0, 4], [16, 4], [0, 2]], 8 * b)
             if me:
                 iota(mt(), [[4, 4], [1, 2], [0, 8]], 0)
-            ts(ki, hm(), add_up(2, 4, 8, ["a2"]), hd[2], A.subtract, A.subtract)
+            ts(ki, hm(), add_up(2, 4, 8, ["a2"], 1.0), hd[2], A.subtract, A.subtract)
             ts(kj, ki, 7, None, A.bitwise_and)
             V(v.tensor_tensor, kx(), kj, m8(), A.add, both=True)
-            o = window(3, kx(), 0.0, "c2")
+            S(hn, cown[2], AF.Copy, scale=-0.5, bias=0.5)
+            S(hb, cown[2], AF.Identity, scale=nbig, bias=hbig)
+            S(kp(), kx(), AF.Identity, bias=hn)
+            o = below(2, "c2")
+            S(dd(), kp(), AF.Abs, scale=-1.0, bias=o, ext=["c2"] if me else [])
+            S(thr[3](0, 64), dd(), AF.Relu, scale=big(0, 1), bias=hb)
             layer(3, ["k2"])
             count(3)
             send("count3")
@@ -621,14 +658,18 @@ def rank_program(g, core, T, topo):
         else:
             posk, nk = refills(2, ["a2", "c2"])
             places(2, posk)
-            layer(3, ["k2"])
+            pick("x5", 0, 64, "x3", 0, 128, lw[2](0, 4), ["k2"])
+            layer(3)
             count(3)
-        total(2, "c2")
-    load("y", "lv", R("vt", 0, 512), T.v[:, :], 2.1, 99.0, ext=["c2" if late else "k2"])
-    quant("vq", 0, 128, "vt", 0)
+            S(R("out2", 131, 132), add_up(2, 1, 4, ["c2"]), AF.Identity, bias=cown[2])
+            S(R("out2", 130, 131), R("out2", 131, 132), AF.Identity, bias=land(2, 4, 5), ext=["a2"])
+            send("sum2")
+    load("y", "lv", R("vt", 0, 512), T.v[:, :], 3.0, 99.0, ext=["c2" if late else "k2"])
     book(2, nk)
-    order(3)
+    if not late:
+        order(3)
     stops(3)
+    quant("vq", 0, 128, "vt", 0, after=signs[-1:] if late else [])
     head(3)
     lo = c0 if me == 3 else c0 + 1
     if rich:
@@ -636,7 +677,7 @@ def rank_program(g, core, T, topo):
         for c in (0, 1):
             V(v.tensor_tensor_scan, pre[c](lo, 9), land(3, lo, 9), mkr[c](lo, 9), 0.0, A.add, A.mult, ext=["a3"])
             ts(lst(c, c + 1), pre[c](8, 9), hc[3] if late else mine(3, smr[c]), clip, A.add, A.max)
-        pick("x4", W4 + 16 * me - (24 if me == 0 else 0), 32, "xq", 0, XQW, lst(), ["pt", "pw", "px"])
+        pick("x4", W4 + 16 * me + (16 if late else -24), 32, "xq", 0, XQW, lst(), ["pt", "pw", "px"])
     else:
         serve(3, ["a3"], lo, "x4", W4 + 16 * me, mine(3), clip if poor else None)
     send("cols3")
@@ -654,14 +695,24 @@ def rank_program(g, core, T, topo):
 
     pick("fin", 0, 48, "cc", 0, 80, lfin())
     S(R("num", 0, 48), by(sidc(), lfin()), AF.Copy)
-    pick("fin", 48, 64, "x4", 0, 192, lw[3](), ["k3"], ["p3"])
-    mm("py", "vq", 0, "fin", 48, True, True)
-    V(v.tensor_copy, R("ys", 0, 64), R("py", 0, 64))
-    for a, b in ((0, 112),) if half else ((0, 48), (48, 112)):
+    if late:
+        yw = F(208)
+        V(v.tensor_copy, words("fin", 48, 112), by(words("x4", 0, 208), lw[3]()), ext=["k3"])
+        V(v.tensor_copy, R("fins", 48, 112), by(R("x4s", 0, 208), lw[3]()), ext=["p3"])
+        mm("py", "vq", 0, "x4", 0, True, True, 208, ext=["k3", "p3"])
+        S(yw(), R("py", 0, 208), AF.Copy, after=signs[-1:], last=COMES["p3"])
+        S(R("ys", 0, 64), by(yw(), lw[3]()), AF.Copy)
+    else:
+        pick("fin", 48, 64, "x4", 0, 192, lw[3](), ["k3"], ["p3"])
+        mm("py", "vq", 0, "fin", 48, True, True)
+        V(v.tensor_copy, R("ys", 0, 64), R("py", 0, 64))
+    for a, b in ((0, 48), (48, 112)):
         store("y", T.oc[:, 4 * a:4 * b], T.fin[:, a:b].bitcast(u8), R("fin", a, b))
+    for a, b in ((0, 112),) if half else ((0, 48), (48, 112)):
         for k in range(4):
-            store("sy"[k % 2] if b > 48 else "y", T.osc[4 * k:4 * k + 4, a:b], T.fins[32 * k:32 * k + 4, a:b], R("fins", a, b))
-    store("y", T.sid[0:1, :], T.num[0:1, 0:112], R("num", 0, 112))
+            store(("yyss" if late else "ssyy" if half else "syyy")[k] if b > 48 else "y",
+                  T.osc[4 * k:4 * k + 4, a:b], T.fins[32 * k:32 * k + 4, a:b], R("fins", a, b), 0.3)
+    store("y", T.sid[0:1, :], T.num[0:1, 0:112], R("num", 0, 112), 0.3)
     store("s", T.y[:, :], T.ys[:, :], R("ys", 0, 64))
 
     Q = {"v": v, "s": s, "t": te, "g": g, "y": sy}
@@ -678,7 +729,7 @@ def rank_program(g, core, T, topo):
 
     for i in arrange(N):
         n = N[i]
-        need(n["q"], [token[d] for d in n["deps"] if d in token and not n["q"] == N[d]["q"] == "t"] + [(e, comes[e]) for e in n["ext"]])
+        need(n["q"], [token[d] for d in n["deps"] if d in token and d not in n["behind"]] + [(e, comes[e]) for e in n["ext"]])
         done = n["fn"]()
         if n["kind"] != "r":
             sem, step = (n["sem"], 16) if n["kind"] == "d" else (n["q"] + "s", 1)

from concourse.bass import DstId, RemoteDMATransfer
from concourse.mybir import dt, AluOpType, AxisListType, ActivationFunctionType

NR, PL, CS, RD = 8, 64, 16, 3
OWN, TWIN, EXTRA, XQW = 384, 896, 960, 976
SHARE, CUT, POOR, RICH = (40, 48), (24, 39), (3, 2), (0, 3)
WCODES = (2, 6, 6, 8)
NCODES = (8, 8, 12)
W4 = 112
CODES = "float8_e4m3fn_x4"
COMES = {"pt": (9.0, 7.2), "pw": 6.0, "a1": (8.2, 8.3), "b1": (8.9, 8.2), "k1": (0, 0, 0, 0, 11.0, 11.0, 10.7, 11.0),
         "a2": (9.6, 10.0, 10.0, 10.0, 10.7, 10.7, 10.9, 10.7), "px": 14.5, "k2": 13.1, "c2": 13.9, "late": 15.9,
         "a3": 16.25, "k3": 17.6, "p3": 19.4}
LEAVES = {"ahead": 2.2, "share": (4.0, 7.3), "count1": 6.8, "cols1": 8.9, "count2": (9.2, 12.3), "extra": 13.0, "cols2": (10.6, 10.8),
          "late2": 13.8, "count3": 14.5, "sum2": 14.9, "cols3": (17.4, 17.5), "end": 19.95}
WAKE, ISSUE, LEAST = 0.13, 0.35, 0.1

SCRATCH = {
    "wt": ("sbuf", [128, 2048], "bfloat16"), "xt": ("sbuf", [128, 1024], "bfloat16"),
    "ut": ("sbuf", [128, 512], "bfloat16"), "vt": ("sbuf", [128, 512], "bfloat16"),
    "fl": ("sbuf", [128, 3600], "float32"), "il": ("sbuf", [128, 256], "int32"), "ol": ("sbuf", [128, 128], "uint16"),
    "bl": ("sbuf", [128, 1536], "bfloat16"), "ys": ("sbuf", [128, 64], "float32"), "num": ("sbuf", [128, 208], "float32"),
    "cnt": ("sbuf", [128, 48], "bfloat16"),
    "ha": ("psum", [128, 512], "float32"), "py": ("psum", [128, 512], "float32"),
}
for _n, _w in (("wc", 512), ("uq", 128), ("ua", 128), ("ub", 128), ("vq", 128), ("xq", XQW), ("cc", 128), ("fin", 176),
               ("x1", 128), ("x2", 192), ("x3", 176), ("x4", 208), ("x5", 128), ("z2", 128), ("z3", 128)):
    SCRATCH[_n] = ("sbuf", [128, _w], CODES)
    SCRATCH[_n + "s"] = ("sbuf", [128, _w], "uint8")
for _t in range(1, RD + 1):
    SCRATCH["at%d" % _t] = ("sbuf", [128, 512], "bfloat16")
    SCRATCH["out%d" % _t] = ("sbuf", [128, 144], "bfloat16")
for _t in range(4):
    SCRATCH["pz%d" % _t] = ("psum", [128, 512], "float32")
SEMAPHORES = ["vs", "ss", "ts", "gs", "lqx", "lu", "lx", "lv", "lw0", "lw1", "st", "loc",
              "pw", "pt", "px", "a1", "a2", "a3", "b1", "c2", "k1", "k2", "k3", "p3"]


def plan(r, cores, topo):
    core = cores[r]

    def quad_of(i):
        return [j for j, d in enumerate(cores) if d in topo.cores_of(cores[i]) or topo.mates(cores[i], d)]

    quad = quad_of(r)
    first = quad_of(0)
    second = [j for j in range(NR) if j not in first]
    me, half = quad.index(r), 0 if r in first else 1
    twin = [j for j in range(NR) if j not in quad and topo.same_plane(core, cores[j]) and topo.die(cores[j]) == topo.die(core)][0]
    mate = [j for j in quad if j != r and cores[j] in topo.cores_of(core)][0]
    eoff = topo.engines(core, cores[twin])
    eon = [e for e in topo.engines(core, cores[mate]) if e not in eoff][::2]

    def call(writes, eon=eon):
        out = []
        for es, ws in ((eoff, [w for w in writes if w[0] != mate]), (eon, [w for w in writes if w[0] == mate])):
            groups = []
            for w in ws:
                same = [x for x in groups if x[0] == w[1:3]]
                if same:
                    same[0][1].append((w[0], w[3]))
                else:
                    groups.append((w[1:3], [(w[0], w[3])]))
            if len(groups) > 1 and len(ws) in (2, 4):
                groups = [(w[1:3], [(w[0], w[3])]) for w in ws]
            groups.sort(key=lambda x: -len(x[1]))
            n = len(es)
            cuts = {0: [], 1: [n], 2: [n // 2] * 2, 3: [n // 2, n // 4, n // 4], 4: [n // 4] * 4}[len(groups)]
            a = 0
            for (key, ds), c in zip(groups, cuts):
                out.append((es[a:a + c], key[0], key[1], ds))
                a += c
        return out

    def both(buf, d, sem, a, b, nc, ns, sems=None):
        return [(4 * nc, (d, sem, (buf, a, nc), (buf, b, nc))), (ns, (d, sems or sem, (buf + "s", a, ns), (buf + "s", b, ns)))]

    def calls(ws, order=None):
        wide = []
        for n, w in ws:
            if n not in wide:
                wide.append(n)
        return [call([w for n, w in ws if n == k]) for k in (sorted(wide, reverse=True) if order else wide)]

    P = {}
    ws = []
    for a in reversed(first):
        if a != r:
            ws += both("xq", a, "pw", OWN, 128 * ((r - a - 5) % NR), WCODES[first.index(a)], 8)
    P["ahead"] = calls(ws, True)
    if half:
        P["ahead"] = P["ahead"][:2] + [call([w for n, w in ws if n == 8 and w[2][0] == k]) for k in ("xqs", "xq")]
    poor = me == POOR[1 - half]
    n = CUT[1 - half] if poor else SHARE[1 - half]
    nc, ns = (WCODES[me], 8) if half else (0, 0)
    share = both("xq", twin, "pt", OWN + nc, TWIN + nc, n - nc, 0)[:1] + both("xq", twin, "pt", OWN + ns, TWIN + ns, 0, n - ns)[1:]
    extra = both("xq", quad_of(twin)[RICH[1 - half]], "px", OWN + n, EXTRA, SHARE[1 - half] - n, SHARE[1 - half] - n) if poor else []
    P["share"], P["extra"] = (calls(share + extra), []) if half else (calls(share), calls(extra))

    def slot(d, s, t):
        others = [j for j in range(NR - 1, -1, -1) if j != d]
        return 16 * t - 16 + (1 if d in second or t == 2 else 0) + others.index(s)

    for t in (1, 2, 3):
        if half:
            ds = [d for d in reversed(quad) if d != r] + (first if t == 1 else []) if t < 3 or me < 3 else []
        else:
            up, down = [d for d in reversed(quad) if d > r], [d for d in quad if d < r]
            near = up + down if me < 3 else []
            far = second[3:] + second[:3] if t < 3 else second
            ds = up + far + down if t == 1 else (far[:3] + near + far[3:] if t == 2 else far + near)
        sem = ("b1", "c2", "a3")[t - 1] if half else "a%d" % t
        src = ("out%d" % t, 63 if t == 1 else 127, 1)
        ws = [(d, "b1" if d < r and not half and t == 1 else sem, src, ("cnt", slot(d, r, t), 1)) for d in ds]
        now = [w for w in ws if w[1] == sem or w[0] == mate]
        P["count%d" % t] = [call(x) for x in (now, [w for w in ws if w not in now]) if x]
    if half and me == 3:
        P["sum2"] = [call([(d, "a3", ("out2", 130 + (d == twin), 1), ("cnt", 39, 1)) for d in first])]
    peers = [quad[(me + e) % 4] for e in range(4)]

    def plain(buf, base, sem, sems=None):
        ws = []
        for e in range(1, 4):
            ws += both(buf, peers[e], sem, base + 16 * me + 4 * e, base + 16 * me + (16 if base and peers[e] == second[3] else 0), 4, 4, sems)
        return calls(ws)

    P["cols1"] = plain("x2", 0, "k1") if half else []
    if half:
        ws = []
        for j in (2, 1, 0):
            if j != me:
                ws += both("x3", quad[j], "k2", 16 * me if me < 3 else 144, 16 * me, NCODES[j], 12)
        P["cols2"] = calls(ws, True)
        P["late2"] = [call([w for n, w in both("x3", quad[3], "k2", 144 + 4 * (3 - me), 16 * me, 4, 16)], eoff)] if me < 3 else []
    else:
        P["cols2"] = plain("x3", 0, "k2")
    if me == RICH[half]:
        order = [1, 2, 3, 0] if me == 0 else [3, 0, 1, 2]
        base = W4 + 16 * half + 16 * me - 8 * order.index(me)
        ws = []
        for e, j in enumerate(order):
            if j != me:
                ws += both("x4", quad[j], "k3", base + 8 * e, W4 + 16 * me, 6, 6, "p3")
        P["cols3"] = calls(ws)
    else:
        P["cols3"] = plain("x4", W4, "k3", "p3")
    return P, quad, twin


def arrange(N):
    for n in reversed(N):
        for d in n["deps"]:
            N[d]["last"] = min(N[d]["last"], n["last"] - WAKE - N[d]["lat"])
    free, order, left = {}, [], [len(n["deps"]) for n in N]
    ready = [i for i, n in enumerate(N) if not left[i]]
    while ready:
        est = {i: max([free.get(N[i]["q"], 0.0), N[i]["from"]] +
                      [N[d]["end"] + (0.0 if d in N[i]["behind"] or N[d]["kind"] == "r" else WAKE) for d in N[i]["deps"]]) for i in ready}
        a = min(ready, key=lambda i: est[i] + N[i]["dur"])
        i = min([j for j in ready if N[j]["q"] == N[a]["q"] and est[j] < est[a] + N[a]["dur"]], key=lambda j: (N[j]["last"], j))
        free[N[i]["q"]] = est[i] + N[i]["dur"]
        N[i]["end"] = est[i] + N[i]["lat"]
        order.append(i)
        ready.remove(i)
        for j in N[i]["next"]:
            left[j] -= 1
            if not left[j]:
                ready.append(j)
    return order


def rank_program(g, core, T, topo):
    rank = T.rank_of(core)
    if rank is None:
        return
    A, AF = AluOpType, ActivationFunctionType
    v, s, te, sy = g.vector, g.scalar, g.tensor, g.sync
    u8, u32 = dt.uint8, dt.uint32
    plans = [plan(r, T.cores, topo) for r in range(NR)]
    P, quad, twin = plans[rank]
    me, half = quad.index(rank), 1 if twin < rank else 0
    rich, poor = me == RICH[half], me == POOR[half]
    late = half == 1 and me == 3
    comes = {}
    for p in plans:
        for cs in p[0].values():
            for c in cs:
                for es, sem, src, ds in c:
                    for d, dst in ds:
                        if d == rank:
                            comes[sem] = comes.get(sem, 0) + len(es)

    N, seen_by, sent = [], {}, [0]

    def when(x):
        return x[rank if len(x) == NR else half] if isinstance(x, tuple) else x

    def R(name, a, b, st=1):
        ap = T[name][:, a:b:st] if st > 1 else T[name][:, a:b]
        psum = SCRATCH[name][0] == "psum"
        return (ap, name, 0 if psum else a, 512 if psum else b, len(range(a, b, st)), None)

    def words(name, a, b):
        return (T[name][:, a:b].bitcast(u32), name, a, b, b - a, None)

    def by(w, off):
        return (w[0].indirect(off[0]), w[1], w[2], w[3], 16 * off[4], off)

    def note(q, kind, fn, outs, ins, dur, lat=None, ext=(), after=(), last=99.0, sem=None, behind=()):
        i = len(N)
        deps = set(after)
        ins = ins + [x[5] for x in outs + ins if x[5]]
        for x, w in [(x, False) for x in ins] + [(x, True) for x in outs]:
            for j, a, b, jw in seen_by.setdefault(x[1], []):
                if (w or jw) and a < x[3] and x[2] < b and j != i:
                    deps.add(j)
            seen_by[x[1]].append((i, x[2], x[3], w))
        behind = [d for d in behind if d not in deps] + [d for d in deps if q == N[d]["q"] == "t"]
        deps |= set(behind)
        ext = [e for e in ext if e in comes]
        N.append({"q": q, "kind": kind, "fn": fn, "deps": sorted(deps), "next": [], "dur": dur, "lat": lat or dur, "ext": ext, "sem": sem,
                  "from": max([0.0] + [when(COMES["late" if late and e == "k2" else e]) for e in ext]), "last": last, "behind": behind})
        for d in deps:
            N[d]["next"].append(i)
        return i

    def op(q, call, *a, outs=1, ext=(), after=(), dur=None, both=False, last=99.0, behind=(), **k):
        views = [x for x in a if isinstance(x, tuple)]
        o = views[:outs] + [k[x] for x in k if x == "accum_out"]
        i = views[outs:] + [k[x] for x in k if x != "accum_out" and isinstance(k[x], tuple)]
        if dur is None:
            n = views[0][4]
            if views[0][5]:
                dur = 0.05 + 0.003 * n
            elif [x for x in i if x[5]]:
                dur = 0.06 + 0.0015 * n
            else:
                dur = max(LEAST, 0.001 * max(x[4] for x in views) * (2 if both else 1))
        a2 = [x[0] if isinstance(x, tuple) else x for x in a]
        k2 = {x: k[x][0] if isinstance(k[x], tuple) else k[x] for x in k}
        return note(q, "c", lambda: call(*a2, **k2), o, i, dur, ext=ext, after=after, last=last, behind=behind)

    def V(call, *a, **k):
        return op("v", call, *a, **k)

    def S(out, in_, f, **k):
        return op("s", s.activation, out, in_, f, **k)

    def ts(out, a, s1, s2, o0, o1=None, **k):
        return V(v.tensor_scalar, out, a, s1, None, o0, **k) if o1 is None else V(v.tensor_scalar, out, a, s1, s2, o0, o1, **k)

    def quant(dst, a, n, src, b, **k):
        return V(v.quantize_mx, R(dst, a, a + n), R(dst + "s", a, a + n), R(src, b, b + 4 * n), outs=2, dur=0.012 + 0.00088 * n, **k)

    def mm(out, w, a, x, b, start, stop, n=128, **k):
        return op("t", te.matmul_mx, R(out, 0, n), R(w, a, a + 128), R(w + "s", a, a + 128), R(x, b, b + n), R(x + "s", b, b + n),
                  start, stop, dur=0.09, **k)

    def iota(out, pattern, base, cm=0):
        k = {} if out[1] == "il" else {"allow_small_or_imprecise_dtypes": True}
        return op("g", g.iota, out, pattern, base, cm, dur=0.13 + 0.002 * out[4], **k)

    def load(q, sem, dst, src, lat, last, **k):
        return note(q, "d", lambda: (s if q == "s" else sy).dma_start(dst[0], src), [dst], [], 0.05, lat, sem=sem, last=last, **k)

    def store(q, dst, src, reads, more=0.0):
        return note(q, "d", lambda: (s if q == "s" else sy).dma_start(dst, src), [], [reads], 0.2, sem="st", last=LEAVES["end"] + more)

    def send(name, after=()):
        for m, c in enumerate(P.get(name, [])):
            def raw(x):
                a = T[x[0]][:, x[1]:x[1] + x[2]]
                return a.bitcast(u8) if SCRATCH[x[0]][2] == CODES else a
            trs = []
            for es, sem, src, ds in c:
                ids = [topo.addr(T.cores[d], core) for d, dst in ds]
                trs.append(RemoteDMATransfer(dst_ids=[DstId(rid=a, pnc=b) for a, b in ids], dma_engine_mask=sum(1 << e for e in es),
                                             remote_sem=T.sem[sem], srcs=[raw(src)], dsts=[raw(dst) for d, dst in ds]))
                sent[0] += len(es)
            note("g", "r", lambda trs=trs: g.remote_dma_fused(trs, local_sem=T.sem.loc), [],
                 [R(x[2][0], x[2][1], x[2][1] + x[2][2]) for x in c], ISSUE, after=after, last=when(LEAVES[name]) + ISSUE * m)

    at = {"fl": 0, "il": 0, "ol": 0, "bl": 0}

    def take(buf, n):
        al = {"fl": 8, "il": 1, "ol": 2, "bl": 16}[buf] if n > 1 or buf == "ol" else 1
        a0 = -(-at[buf] // al) * al
        at[buf] = a0 + n
        return lambda a=0, b=n, st=1: R(buf, a0 + a, a0 + b, st)

    def F(n=1):
        return take("fl", n) if n > 1 else take("fl", 1)()

    def I(n=1):
        return take("il", n)()

    def O(n=1):
        return take("ol", n)

    def pick(dst, a, n, src, lo, hi, lst, ext=(), exts=None, behind=()):
        V(v.tensor_copy, words(dst, a, a + n), by(words(src, lo, hi), lst), ext=ext, behind=behind)
        S(R(dst + "s", a, a + n), by(R(src + "s", lo, hi), lst), AF.Copy, ext=exts or ext)

    load("s", "lu", R("ut", 0, 8), T.u[:, 0:8], 1.6, -5.0)
    load("y", "lqx", R("xt", 256, 448), T.qx[:, 0:192], 1.9, -5.0)
    load("s", "lw0", R("wt", 0, 1536), T.w[:, 0:1536], 3.0, -4.0)
    load("y", "lx", R("xt", 0, 256), T.x[:, :], 3.2, -4.0)
    load("y", "lw1", R("wt", 1536, 2048), T.w[:, 1536:2048], 3.8, -3.0)

    ip, ip2, neg, rs0, long = I(), I(), F(3), F(64), F(128)
    iota(ip, [[0, 1]], 0, 1)
    iota(ip2, [[0, 1]], 4 * me, 1)
    iota(rs0(), [[0, 4], [1, 16]], 0)
    if me < 3:
        iota(neg(0, 3 - me), [[1, 3 - me]], -3)
    if me > 0:
        iota(neg(3 - me, 3), [[1, me]], 1 - me)
    iota(long(48 if half else 0, 128), [[1, 80 if half else 128]], 0 if half else -48)

    def row(a=0, b=80):
        return long(48 + a, 48 + b)

    krow = rs0(0, 16)
    V(v.memset, R("xt", 448, 1024), 0.0, dur=0.3)
    lua, lw = O(8), {1: O(5), 2: O(5), 3: O(4)}
    V(v.memset, lua(), 0)
    caps, mk, seed = take("bl", 192), F(9), F(16)

    def c16(a=0, b=128):
        return caps(64 + a, 64 + b)

    V(v.memset, seed(), 2.0 ** 60)
    fills, later = [quant("x2", 0, 128, "xt", 448)], []
    (fills if half or me == 3 else later).append(quant("x3", 0, 176, "xt", 256))
    later.append(quant("x4", 0, 128, "xt", 448))
    quant("cc", 0, 128, "xt", 448)
    if late:
        later.append(quant("x4", 80, 128, "xt", 256))
        quant("x5", 0, 128, "xt", 256)
        S(R("at3", 256, 512), R("xt", 448, 704), AF.Copy)
    else:
        quant("fin", 48, 128, "xt", 256)
    ik, kcol, kcol2, ic, dcol, ih, isl, b3, hc0a, hc0, sm, m16 = I(), F(), F(), I(), F(), I(), I(), I(), F(), F(), F(), F(64)
    ts(ik, ip, 15, None, A.bitwise_and)
    ts(ic, ip2, 2, 3, A.logical_shift_right, A.bitwise_and)
    ts(ih, ip, 1, 1, A.logical_shift_right, A.bitwise_and)
    ts(isl, ip, 1, None, A.bitwise_and)
    ts(b3, ip, 3, 1, A.logical_shift_right, A.bitwise_and)
    V(v.tensor_copy, kcol, ik)
    V(v.tensor_copy, dcol, ic)
    ts(kcol2, b3, 400.0, kcol, A.mult, A.add)
    loc = (TWIN, OWN) if half else (OWN, TWIN)
    ts(hc0a, ih, loc[1] - loc[0] - 0.5, loc[0] + (3.5 - me) / 8.0, A.mult, A.add)
    c0 = 1 if half else 4
    V(v.memset, mk(0, 8), 1.0)
    V(v.memset, mk(8, 9), 0.125)
    ts(sm, dcol, float(me), 0.125, A.is_gt, A.mult)
    ts(mk(c0, c0 + 3), neg(), dcol, 0.0, A.add, A.is_gt)
    ts(hc0, isl, hc0a, None, A.add)
    ts(m16(), rs0(), kcol, None, A.is_equal)
    for t in (1, 2):
        V(v.memset, lw[t](4, 5), 448 - 128 * t)
    wants = take("bl", 336)
    want = {t: (lambda a, b, o=o: wants(o + a, o + b)) for t, o in ((1, 256), (2, 0), (3, 256 if late else 128))}
    S(R("ut", 8, 512), R("xt", 448, 952), AF.Copy)
    S(R("at1", 256, 512), R("xt", 448, 704), AF.Copy)
    big, rst, kh, hbig, nbig, k512, jw = F(16), F(64), F(), F(), F(), F(16), F(3)
    S(big(), seed(), AF.Square)
    bigb = take("bl", 1)()
    S(bigb, big(0, 1), AF.Copy)
    S(rst(), rs0(), AF.Sign)
    S(kh, kcol, AF.Copy, bias=0.5)
    if half and not late:
        S(hbig, big(0, 1), AF.Copy, scale=0.5)
        S(nbig, big(0, 1), AF.Copy, scale=-0.5)
    S(k512(), krow, AF.Copy, bias=float(NR * PL))
    S(jw(), long(48, 96, 16), AF.Identity, bias=kcol)

    def num(a=0, b=80):
        return R("num", 48 + a, 48 + b)

    sidc, lrow, thr = (lambda a=0, b=80: R("num", 128 + a, 128 + b)), {1: F(80), 2: F(80), 3: row}, {2: F(144), 3: F(144)}
    S(num(0, 64), row(0, 64), AF.Copy, bias=float(PL * rank))
    S(R("num", 112, 208), R("xt", 448, 544), AF.Copy, bias=-1.0)
    wide = {2: not half, 3: half and not late}
    for t in (2, 3):
        if not (late and t == 3):
            S(thr[t](64, 144), R("xt", 448, 528), AF.Copy)
            if not wide[t]:
                S(thr[t](0, 64), R("xt", 448, 512), AF.Identity, bias=big(0, 1))
    V(v.memset, R("cnt", 8, 48, 16), 0.0)
    V(v.memset, wants(320, 336), 1.0)
    for t in (1, 2):
        S(lrow[t](), row(), AF.Copy, bias=64.0)
    S(c16(), R("xt", 448, 576), AF.Copy, bias=16.0)
    hp = POOR[half] + 4 * (1 - half)
    pt, n8 = F(800), 8 * SHARE[half]
    iota(pt(0, 64), [[0, 8], [2, 2], [16, 4]], 0)
    for a, b in ((64, 128), (128, 256), (256, n8)):
        S(pt(a, b), pt(0, b - a), AF.Copy)
    V(v.memset, pt(8 * CUT[half] + hp, n8, 8), 16.0 * RICH[half] + 4)
    S(pt(400, 400 + n8), pt(0, n8), AF.Copy, bias=1.0)

    quant("xq", OWN, 128, "xt", 256)
    send("ahead")
    if not half:
        send("share")
    S(R("ut", 128, 132), R("ut", 4, 8), AF.Copy, scale=-1.0)
    quant("uq", 0, 128, "ut", 0)
    pick("ub", 0, 128, "uq", 32, 128, lua())
    pick("ua", 0, 128, "uq", 0, 128, lua())
    quant("x1", 0, 128, "xt", 0)
    for i in range(4):
        quant("wc", 128 * i, 128, "wt", 512 * i)

    sat = {t: take("bl", 80) for t in (2, 3)}
    sat[1] = lambda: R("out1", 0, 80)
    cown = {t: R("out%d" % t, 63 if t == 1 else 127, 64 if t == 1 else 128) for t in (1, 2, 3)}
    logo = {t: O() for t in (1, 2, 3)}
    hd, hc, signs = {}, {1: hc0}, []

    def land(t, a, b):
        return R("cnt", 16 * t - 16 + a, 16 * t - 16 + b)

    def layer(t, ext=()):
        n = 64 if t == 1 or late and t == 3 else 128
        for i in range(4):
            mm("pz%d" % i, "wc", 128 * i, "x5" if late and t == 3 else "x%d" % t, 0, True, True, ext=ext)
        for i in range(4):
            o, z = R("at%d" % t, i, 4 * n, 4), R("pz%d" % i, 0, n)
            o = o[:1] + ("at%d.%d" % (t, i),) + o[2:]
            if i % 2:
                ts(o, z, 0.0, 0.0625, A.max, A.mult)
            else:
                S(o, z, AF.Relu, scale=0.0625)
        dst, a = ("x2", 64) if t == 1 else ("x4", 0) if late and t == 3 else ("z%d" % t, 0)
        j = len(N)
        V(v.quantize_mx, R(dst, a, a + 128), R(dst + "s", a, a + 128), R("at%d" % t, 0, 512), outs=2, dur=0.125, after=range(j - 4, j))
        mm("ha", "ua", 0, dst, a, True, False)
        mm("ha", "ub", 0, dst, a, False, True)

    def count(t, cap=c16):
        if t == 1 or late and t == 3:
            ts(want[t](0, 64), R("ha", 0, 64), 0.0, None, A.is_gt)
            return V(v.tensor_tensor_scan, sat[t](), want[t](0, 80), c16(0, 80), 0.0, A.add, A.min)
        V(v.tensor_tensor, want[t](0, 128), R("ha", 0, 128), thr[t](0, 128), A.is_gt)
        return V(v.tensor_tensor_scan, R("out%d" % t, 0, 128), want[t](0, 128), cap(), 0.0, A.add, A.min, dur=LEAST)

    def stops(t):
        wg, red = take("bl", 80), F()
        if t > 1 and not (late and t == 3):
            S(wg(), by(want[t](0, 592 - 128 * t), lw[t - 1]()), AF.Copy)
            V(v.tensor_tensor_scan, sat[t](), wg(), c16(0, 80), 0.0, A.add, A.min)
        signs.append(S(F(80)(), sat[t](), AF.Sign, bias=kh, scale=-1.0, accum_out=red))
        ts(logo[t](), red, 0.5, 40.0, A.mult, A.add)

    def add_up(t, a, b, ext, wait=0.0):
        o = F()
        N[S(F(8)(0, b - a), land(t, a, b), AF.Identity, accum_out=o, ext=ext)]["from"] += wait
        return o

    def head(t):
        hd[t], hc[t], o = F(), F(), F()
        a, b = (1, 8) if half else (0, 7) if t == 2 else (5 if me == 3 else 6, 8)
        tot = add_up(t - 1, a, b, ["a1", "b1"] if t == 2 else ["a2", "c2"])
        if t == 2:
            S(hd[t], tot, AF.Identity, bias=cown[1])
        else:
            S(o, cown[2], AF.Identity, bias=hd[2])
            S(hd[t], tot, AF.Identity, bias=o)
        S(hc[t], hd[t], AF.Identity, scale=0.125, bias=hcr if rich and t == 3 else hc0)

    def mine(t, m=sm):
        o = F()
        S(o, cown[t], AF.Identity, scale=m, bias=hc[t])
        return o

    def serve(t, ext, lo, dst, a, h, clip=None):
        pre, lst = F(9), O()
        if t == 2 and not half:
            V(v.tensor_tensor_scan, pre(lo, 8), land(t, lo, 8), mk(lo - 1, 7), 0.0, A.add, A.mult, ext=ext)
            ts(lst(), pre(7, 8), 0.125, h, A.mult, A.add)
        else:
            V(v.tensor_tensor_scan, pre(lo, 9), land(t, lo, 9), mk(lo, 9), 0.0, A.add, A.mult, ext=ext)
            if clip is None:
                ts(lst(), pre(8, 9), h, None, A.add)
            else:
                ts(lst(), pre(8, 9), h, clip, A.add, A.min)
        pick(dst, a, 16, "xq", 0, EXTRA, lst(), ["pt", "pw"])

    def refills(t, ext, o=None):
        lp, l2, mrow, posk, nk, st = O(), O(), F(16), F(16), F(16), F()
        pr = add_up(t, c0 + 3 - me + (t == 2 and not half), 8, ext) if half or me or t == 3 else None
        k = kcol2 if o is None else kcol
        if t == 1 or pr is None:
            st = pr or hd[t]
            ts(lp(), k, st, None, A.add, ext=ext)
        else:
            ts(lp(), k, pr, hd[t], A.add, A.add)
            S(st, pr, AF.Identity, bias=hd[t])
        if o is None:
            S(posk(), by(pt(), lp()), AF.Copy, bias=float(W4 + 16 * late if t == 3 else 0))
        else:
            ts(l2(), kcol, o, None, A.add, ext=ext)
            S(mrow(), by(mt(), l2()), AF.Copy)
            V(v.tensor_tensor, posk(), by(pt(), lp()), mrow(), A.add)
        S(nk(), k512(), AF.Identity, bias=st)
        return posk, nk

    def places(t, posk):
        lm, sg = F(64), F(64)
        V(v.tensor_copy, by(lrow[t](), logo[t]()), posk())
        V(v.tensor_tensor, lm(), lrow[t](0, 64), m16(), A.mult, both=True)
        V(v.tensor_tensor_scan, sg(), rst(), lm(), 0.0, A.mult, A.add)
        V(v.tensor_copy, lw[t](0, 4), sg(15, 64, 16))

    def gate(t, posk):
        dg, pw, lg, vk = F(16), F(), O(), F(16)
        V(v.tensor_copy, by(thr[t](64, 144), logo[t - 1]()), big())
        V(v.tensor_tensor, dg(), posk(), m16(0, 16), A.mult)
        S(F(16)(), dg(), AF.Identity, accum_out=pw)
        V(v.tensor_copy, lg(), pw)
        ts(vk(), krow, cown[t - 1], bigb, A.is_ge, A.mult)
        V(v.tensor_copy, by(thr[t](0, 64), lg()), vk())

    def order(t):
        pick("x%d" % (t + 1), 64 if t < 3 else 0, 64, "z%d" % t, 0, 128, lw[t - 1](0, 4))

    def book(t, nk):
        s0 = 64 if t < 3 else 0
        pick("cc", 16 * t - 16, 16, "x%d" % (t + 1), s0, s0 + 80, logo[t]())
        S(sidc(16 * t - 16, 16 * t), by(num(), logo[t]()), AF.Copy)
        V(v.tensor_copy, by(num(), logo[t]()), nk())
        if t < 3:
            S(num(64, 80), R("xt", 448, 464), AF.Copy, bias=-1.0)

    def below(t, sem):
        V(v.tensor_copy, by(thr[t + 1](64, 144), logo[t]()), big())
        if me < 2:
            return land(t, c0 + 2, c0 + 3) if me else 0.0
        if me == 3:
            return add_up(t, c0, c0 + 3, [sem])
        o = F()
        S(o, land(t, c0 + 1, c0 + 2), AF.Identity, bias=land(t, c0 + 2, c0 + 3), ext=[sem])
        return o

    clip, hcr, mkr, smr = F(), F(), [F(9), F(9)], [F(), F()]
    if poor:
        top = TWIN + CUT[half] - 1.0
        ts(clip, ih, (top - 4095.0) * (-1 if half else 1), top if half else 4095.0, A.mult, A.add)
    if rich:
        mark = len(N)
        turn = [1, 2, 3, 0] if me == 0 else [3, 0, 1, 2]
        i3, t1, t2, t3 = I(), F(), F(), F()
        v0, v1, v2 = loc[0] + (3.5 - me) / 8.0, loc[1] + (3.5 - me - 4) / 8.0, EXTRA - CUT[half] + (3.5 - hp) / 8.0
        ts(i3, ip, 1, 3, A.logical_shift_right, A.bitwise_and)
        for c in (0, 1):
            d = F()
            S(mkr[c](), mk(), AF.Copy)
            ts(d, b3, float(turn[2 * c + 1] - turn[2 * c]), float(turn[2 * c]), A.mult, A.add)
            ts(mkr[c](c0, c0 + 3), neg(), d, 0.0, A.add, A.is_gt)
            if not late:
                ts(smr[c], d, float(me), 0.125, A.is_gt, A.mult)
        ts(t1, i3, 1.0, v1 - v0, A.is_equal, A.mult)
        ts(t2, i3, 2.0, v2 - v0, A.is_equal, A.mult)
        ts(clip, i3, 2.0, float(EXTRA), A.is_equal, A.mult)
        ts(t3, isl, t1, t2, A.add, A.add)
        S(hcr, t3, AF.Copy, bias=v0)
        for n in N[mark:] if not late else []:
            n["from"] = 13.5

    layer(1)
    counted = count(1)
    send("count1", fills)
    if half:
        send("share", [len(N) - 1])
    stops(1)
    if not half:
        ipw, two, wa, wc0, wc1, lwin, posk, nk = I(), F(4), I(), F(), F(), O(4), F(16), F(16)
        iota(ipw, [[0, 1]], NR - 5 - me, 1)
        iota(two(), [[2, 4]], 0)
        ts(wa, ipw, 7, None, A.bitwise_and)
        ts(wc0, wa, 128.0, None, A.mult)
        ts(wc1, b3, wc0, None, A.add)
        ts(lwin(), two(), wc1, None, A.add)
        w0, ext = 48 - 16 * me, ["a1"] if me else []
        pick("x2", w0, 64 - w0, "xq", 0, TWIN + WCODES[me], lwin(0, me + 1), ["pw"], behind=[counted])
        kq, hq = F(64), F()
        S(hq, cown[1], AF.Copy, scale=-1.0, bias=0.5 - w0)
        S(kq(), row(0, 64), AF.Identity, bias=hq)
        o = below(1, "a1")
        ts(thr[2](0, 64), kq(), o, bigb if me == 1 else big(0, 1), A.is_gt, A.mult, ext=ext)
        ts(caps(0, 64), row(-w0, 64 - w0), o, 16.0, A.is_ge, A.mult, ext=ext)
        layer(2)
        count(2, lambda: caps(0, 128))
        send("count2", later)
        S(posk(), row(w0, w0 + 16), AF.Identity, bias=o, ext=ext)
        S(nk(), k512(), AF.Identity, bias=o, ext=ext)
        places(1, posk)
        book(1, nk)
        head(2)
        order(2)
        stops(2)
        serve(2, ["a2"], c0 + 1 if me == 3 else c0 + 2, "x3", 16 * me, mine(2))
        send("cols2")
        send("extra", [len(N) - 1])
        posk, nk = refills(2, ["a2"])
        places(2, posk)
        mark = len(N)
        gate(3, posk)
        for n in N[mark:]:
            n["from"] = when(LEAVES["cols2"])
        layer(3, ["k2"])
        count(3)
        send("count3")
    else:
        e4, hcn, hcn2 = I(), F(), F()
        ts(e4, ip, 2, 3, A.logical_shift_right, A.bitwise_and)
        ts(hcn, e4, 2.0, hc0, A.mult, A.add)
        serve(1, ["a1", "b1"], c0, "x2", 16 * me, mine(1))
        send("cols1")
        posk, nk = refills(1, ["a1", "b1"])
        places(1, posk)
        book(1, nk)
        head(2)
        S(hcn2, hd[2], AF.Identity, scale=0.125, bias=hcn)
        serve(2, ["a2"], 4, "x3", 144 if late else 16 * me, hcn2)
        send("cols2")
        gate(2, posk)
        layer(2, ["k1"])
        order(2)
        count(2)
        send("count2", later)
        stops(2)
        serve(2, ["a2", "c2"], c0, "x3", 48 if late else 144, mine(2))
        send("late2")
        if not late:
            hm, m8, mt, ki, kj, kx, hn, hb, kp, dd = F(64), F(64), F(64), I(64), I(64), F(64), F(), F(), F(64), F(64)
            for b in (0, 1):
                iota(hm(b, 64, 2), [[1, 4], [0, 4], [4, 2]], 512)
                iota(m8(b, 64, 2), [[0, 4], [16, 4], [0, 2]], 8 * b)
            if me:
                iota(mt(), [[4, 4], [1, 2], [0, 8]], 0)
            ts(ki, hm(), add_up(2, 4, 8, ["a2"], 1.0), hd[2], A.subtract, A.subtract)
            ts(kj, ki, 7, None, A.bitwise_and)
            V(v.tensor_tensor, kx(), kj, m8(), A.add, both=True)
            S(hn, cown[2], AF.Copy, scale=-0.5, bias=0.5)
            S(hb, cown[2], AF.Identity, scale=nbig, bias=hbig)
            S(kp(), kx(), AF.Identity, bias=hn)
            o = below(2, "c2")
            S(dd(), kp(), AF.Abs, scale=-1.0, bias=o, ext=["c2"] if me else [])
            S(thr[3](0, 64), dd(), AF.Relu, scale=big(0, 1), bias=hb)
            layer(3, ["k2"])
            count(3)
            send("count3")
            posk, nk = refills(2, ["a2", "c2"] if me else ["a2"], o if me else None)
            places(2, posk)
        else:
            posk, nk = refills(2, ["a2", "c2"])
            places(2, posk)
            pick("x5", 0, 64, "x3", 0, 128, lw[2](0, 4), ["k2"])
            layer(3)
            count(3)
            S(R("out2", 131, 132), add_up(2, 1, 4, ["c2"]), AF.Identity, bias=cown[2])
            S(R("out2", 130, 131), R("out2", 131, 132), AF.Identity, bias=land(2, 4, 5), ext=["a2"])
            send("sum2")
    load("y", "lv", R("vt", 0, 512), T.v[:, :], 3.0, 99.0, ext=["c2" if late else "k2"])
    book(2, nk)
    if not late:
        order(3)
    stops(3)
    quant("vq", 0, 128, "vt", 0, after=signs[-1:] if late else [])
    head(3)
    lo = c0 if me == 3 else c0 + 1
    if rich:
        pre, lst = [F(9), F(9)], O(2)
        for c in (0, 1):
            V(v.tensor_tensor_scan, pre[c](lo, 9), land(3, lo, 9), mkr[c](lo, 9), 0.0, A.add, A.mult, ext=["a3"])
            ts(lst(c, c + 1), pre[c](8, 9), hc[3] if late else mine(3, smr[c]), clip, A.add, A.max)
        pick("x4", W4 + 16 * me + (16 if late else -24), 32, "xq", 0, XQW, lst(), ["pt", "pw", "px"])
    else:
        serve(3, ["a3"], lo, "x4", W4 + 16 * me, mine(3), clip if poor else None)
    send("cols3")
    posk, nk = refills(3, ["a3"])
    places(3, posk)
    book(3, nk)
    d0, n2, d1, g1, g2, lfin = take("bl", 1)(), F(), F(), F(3), F(3), O(3)
    S(d0, cown[1], AF.Copy, scale=-1.0, bias=16.0)
    S(n2, cown[1], AF.Identity, bias=cown[2])
    S(d1, cown[2], AF.Copy, scale=-1.0, bias=16.0)
    ts(g1(), jw(), cown[1], d0, A.is_ge, A.mult)
    ts(g2(), jw(), n2, d1, A.is_ge, A.mult)
    for c in range(3):
        ts(lfin(c, c + 1), jw(c, c + 1), g1(c, c + 1), g2(c, c + 1), A.add, A.add)

    pick("fin", 0, 48, "cc", 0, 80, lfin())
    S(R("num", 0, 48), by(sidc(), lfin()), AF.Copy)
    if late:
        yw = F(208)
        V(v.tensor_copy, words("fin", 48, 112), by(words("x4", 0, 208), lw[3]()), ext=["k3"])
        V(v.tensor_copy, R("fins", 48, 112), by(R("x4s", 0, 208), lw[3]()), ext=["p3"])
        mm("py", "vq", 0, "x4", 0, True, True, 208, ext=["k3", "p3"])
        S(yw(), R("py", 0, 208), AF.Copy, after=signs[-1:], last=COMES["p3"])
        S(R("ys", 0, 64), by(yw(), lw[3]()), AF.Copy)
    else:
        pick("fin", 48, 64, "x4", 0, 192, lw[3](), ["k3"], ["p3"])
        mm("py", "vq", 0, "fin", 48, True, True)
        V(v.tensor_copy, R("ys", 0, 64), R("py", 0, 64))
    for a, b in ((0, 48), (48, 112)):
        store("y", T.oc[:, 4 * a:4 * b], T.fin[:, a:b].bitcast(u8), R("fin", a, b))
    for a, b in ((0, 112),) if half else ((0, 48), (48, 112)):
        for k in range(4):
            store(("yyss" if late else "ssyy" if half else "syyy")[k] if b > 48 else "y",
                  T.osc[4 * k:4 * k + 4, a:b], T.fins[32 * k:32 * k + 4, a:b], R("fins", a, b), 0.3)
    store("y", T.sid[0:1, :], T.num[0:1, 0:112], R("num", 0, 112), 0.3)
    store("s", T.y[:, :], T.ys[:, :], R("ys", 0, 64))

    Q = {"v": v, "s": s, "t": te, "g": g, "y": sy}
    counts, token, seen = {}, {}, {q: {} for q in Q}

    def need(q, deps):
        top = {}
        for n, c in deps:
            top[n] = max(top.get(n, 0), c)
        for n, c in top.items():
            if seen[q].get(n, 0) < c:
                Q[q].wait_ge(T.sem[n], c)
                seen[q][n] = c

    for i in arrange(N):
        n = N[i]
        need(n["q"], [token[d] for d in n["deps"] if d in token and d not in n["behind"]] + [(e, comes[e]) for e in n["ext"]])
        done = n["fn"]()
        if n["kind"] != "r":
            sem, step = (n["sem"], 16) if n["kind"] == "d" else (n["q"] + "s", 1)
            done.then_inc(T.sem[sem], step)
            counts[sem] = counts.get(sem, 0) + step
            token[i] = (sem, counts[sem])
    need("g", list(counts.items()) + [("loc", sent[0])] + list(comes.items()))
